import numpy as np
import ml_dtypes


def mxq(x, axis, fmt="e4m3"):
    dtype, down = {"e4m3": (ml_dtypes.float8_e4m3fn, 7), "e5m2": (ml_dtypes.float8_e5m2, 14)}[fmt]
    v = np.moveaxis(np.asarray(x, np.float32).astype(ml_dtypes.bfloat16).astype(np.float64), axis, -1)
    blocks = v.reshape(v.shape[:-1] + (-1, 32))
    amax = np.abs(blocks).max(-1, keepdims=True)
    byte = np.maximum(np.where(amax > 0, np.frexp(amax)[1] - 1 + 127, 0) - down, 1)
    scale = np.exp2(byte - 127.0)
    codes = (blocks / scale).astype(np.float32).astype(dtype).astype(np.float64)
    return np.moveaxis((codes * scale).reshape(v.shape), -1, axis)


WIDE = False


def mx_kscale(k):
    if not WIDE:
        return np.ones(k)
    levels = np.array([10, -10, 5, -5, 0])
    if k % 512:
        return np.exp2(np.random.permutation(np.resize(levels, k // 32))).repeat(32)
    a = np.empty((k // 512, 16))
    for p in range(k // 512):
        a[p, :8] = np.random.permutation(np.resize(levels, 8))
        for g in range(8):
            far = levels[np.abs(levels - a[p, g]) >= 10]
            a[p, g + 8] = far[np.random.randint(len(far))]
    return np.exp2(a.ravel()).repeat(32)


def f64(x):
    return np.asarray(x).astype(np.float64)


def striped(idx):
    return np.tile(idx.reshape(-1, 16).T, (8, 1)).astype(np.uint16)


def unstriped(offs):
    return offs[:16].T.reshape(-1).astype(np.int64)


E2M1 = np.array([0.0, 0.5, 1.0, 1.5, 2.0, 3.0, 4.0, 6.0, -0.0, -0.5, -1.0, -1.5, -2.0, -3.0, -4.0, -6.0])


def pack_weight(w, fmt):
    k, n = w.shape
    w = f64(np.asarray(w, np.float32).astype(ml_dtypes.bfloat16)).reshape(k // 32, 32, n)
    amax = np.abs(w).max(1)
    if fmt == "e4m3":
        byte = np.frexp(amax)[1] - 1 + 127 - 7
    else:
        mant, ex = np.frexp(amax / 6.0)
        byte = np.where(mant > 0.5, ex, ex - 1) + 127
    byte = np.clip(np.where(amax > 0, byte, 1), 1, 254)
    scaled = (w * np.exp2(127.0 - byte)[:, None, :]).reshape(k, n).astype(np.float32)
    by_word = np.ascontiguousarray(scaled.reshape(k // 512, 128, 4, n).transpose(0, 1, 3, 2))
    if fmt == "e4m3":
        words = by_word.astype(ml_dtypes.float8_e4m3fn).view(np.uint8)
    else:
        c = by_word.astype(ml_dtypes.float4_e2m1fn).view(np.uint8) & 0xF
        words = (c[..., 0::2] | (c[..., 1::2] << 4)).reshape(k // 512, 128, 2 * n)
    return np.ascontiguousarray(words), np.ascontiguousarray(byte.astype(np.uint8).reshape(k // 512, 16, n))


def unpack_weight(words, scales, fmt):
    g, _, n = scales.shape
    words = np.ascontiguousarray(words).reshape(g, 128, n, -1)
    if fmt == "e4m3":
        vals = words.view(ml_dtypes.float8_e4m3fn).astype(np.float64)
    else:
        nib = np.empty((g, 128, n, 4), np.uint8)
        nib[..., 0::2] = words & 0xF
        nib[..., 1::2] = words >> 4
        vals = E2M1[nib]
    vals = vals * np.repeat(np.exp2(scales.astype(np.float64) - 127.0), 8, axis=1)[..., None]
    return vals.transpose(0, 1, 3, 2).reshape(g * 512, n)


def gelu(v):
    return 0.5 * v * (1.0 + np.tanh(np.sqrt(2.0 / np.pi) * (v + 0.044715 * v**3)))


K, H, N, T, S = 1024, 512, 512, 2048, 1024


def setup_inputs():
    n = np.random.standard_normal
    s = mx_kscale(K)[:, None]
    u = mx_kscale(H)[:, None]
    tab_words, tab_scales = pack_weight(n((K, T)) * s, "e2m1")
    wi_words, wi_scales = pack_weight(n((K, H)) / np.sqrt(K) / s, "e4m3")
    wrel_words, wrel_scales = pack_weight(n((H, N)) / np.sqrt(H) / u, "e2m1")
    return {
        "tab_words": tab_words, "tab_scales": tab_scales,
        "offs": striped(np.random.permutation(T)[:S]),
        "offs2": striped(np.random.permutation(T)[:S]),
        "wr": (n((K, H)) / np.sqrt(K) / s).astype(np.float32),
        "wi_words": wi_words, "wi_scales": wi_scales,
        "gain": (np.exp(0.3 * n(H)) * u[:, 0]).astype(np.float32),
        "wrel_words": wrel_words, "wrel_scales": wrel_scales,
        "bias": (0.5 * n(N)).astype(np.float32),
    }


def reference(tab_words, tab_scales, offs, offs2, wr, wi_words, wi_scales,
              gain, wrel_words, wrel_scales, bias):
    TW = unpack_weight(tab_words, tab_scales, "e2m1")
    v = TW[:, unstriped(offs)]
    v2 = TW[:, unstriped(offs2)]
    wrq = mxq(f64(wr), 0, "e4m3")
    wi = unpack_weight(wi_words, wi_scales, "e4m3")
    hre = wrq.T @ v
    him = wi.T @ v
    tre = wrq.T @ v2
    tim = wi.T @ v2
    h = (hre * tre + him * tim) * f64(gain)[:, None]
    wrel = unpack_weight(wrel_words, wrel_scales, "e2m1")
    y = wrel.T @ mxq(h, 0, "e4m3")
    return y + f64(bias)[:, None]

@@ -1,0 +1,278 @@
+from contextlib import ExitStack
+
+import concourse.mybir as mybir
+
+K, H, N, T, S = 1024, 512, 512, 2048, 1024
+FLOPS = 2 * (4 * K * H * S + H * N * S)
+
+F32 = mybir.dt.float32
+BF16 = mybir.dt.bfloat16
+I32 = mybir.dt.int32
+U16 = mybir.dt.uint16
+U8 = mybir.dt.uint8
+FP8X4 = mybir.dt.float8_e4m3fn_x4
+FP4X4 = mybir.dt.float4_e2m1fn_x4
+MULT = mybir.AluOpType.mult
+ADD = mybir.AluOpType.add
+COPY = mybir.ActivationFunctionType.Copy
+IDENTITY = mybir.ActivationFunctionType.Identity
+
+P = 128
+PACK = 4
+PASSES = K // (P * PACK)
+CHUNK = 512
+STRIP = 128
+LIST_ROWS = 16
+ALIGN = 64
+SCORE_GROUPS = ((0, 512), (512, 256), (768, 128), (896, 128))
+
+
+def tile_list_complex_kinship_scores_kernel(
+    tc, tab_words, tab_scales, offs, offs2, wr, wi_words, wi_scales, gain, wrel_words, wrel_scales, bias, out
+):
+    nc = tc.nc
+    with ExitStack() as ctx:
+        lists = ctx.enter_context(tc.tile_pool(name="lists", bufs=1))
+        keep = ctx.enter_context(tc.tile_pool(name="keep", bufs=1))
+        psum = ctx.enter_context(tc.psum_pool(name="psum", bufs=8))
+
+        def held(shape, dtype, name, tag=None):
+            return keep.tile(shape, dtype, name=name, tag=tag or name, align_bytes=ALIGN)
+
+        head_list = lists.tile([P, S // LIST_ROWS], U16, name="head_list")
+        tail_list = lists.tile([P, S // LIST_ROWS], U16, name="tail_list")
+
+        table_scales = held([P, T], U8, "table_scales")
+        wi_scales_raw = held([P, PASSES * H], U8, "wi_scales_raw")
+        second_plane = {}
+        for side, first, count in (("tail", 0, CHUNK), ("tail", CHUNK, CHUNK), ("head", 0, S)):
+            second_plane[side, first] = held([P, count], U8, "second_plane_%s%d" % (side, first))
+        nc.gpsimd.memset(table_scales[:].bitcast(I32), 0)
+        nc.gpsimd.memset(wi_scales_raw[:].bitcast(I32), 0)
+        for key in second_plane:
+            nc.gpsimd.memset(second_plane[key][96:P, :].bitcast(I32), 0)
+
+        nc.sync.dma_start(tail_list[:], offs2)
+        for q in range(4):
+            nc.sync.dma_start(
+                table_scales[32 * q : 32 * q + 8, :].bitcast(I32), tab_scales[:, 4 * q : 4 * q + 4, :].bitcast(I32)
+            )
+        table_words = [held([P, T], U16, "table_words%d" % a) for a in range(PASSES)]
+        for a in range(PASSES):
+            nc.sync.dma_start(table_words[a][:].bitcast(I32), tab_words[a].bitcast(I32))
+        wi_raw = held([P, PASSES * H], I32, "wi_raw")
+        nc.sync.dma_start(
+            wi_raw[:].rearrange("p (a c) -> p a c", a=PASSES),
+            wi_words.rearrange("a p c i -> p a (c i)").bitcast(I32),
+        )
+        for q in range(4):
+            nc.gpsimd.dma_start(
+                wi_scales_raw[32 * q : 32 * q + 4, :].bitcast(I32).rearrange("r (a c) -> r a c", a=PASSES),
+                wi_scales[:, 4 * q : 4 * q + 4, :].bitcast(I32).rearrange("a r c -> r a c"),
+            )
+        wr_raw = [held([P, PACK, H], F32, "wr_raw%d" % a) for a in range(PASSES)]
+        for a in range(PASSES):
+            nc.sync.dma_start(wr_raw[a][:], wr[512 * a : 512 * (a + 1), :].rearrange("(p j) c -> p j c", j=PACK))
+        nc.sync.dma_start(head_list[:], offs)
+
+        def gather_words(side, a, first, count, dest):
+            which = tail_list if side == "tail" else head_list
+            cols = slice(first // LIST_ROWS, (first + count) // LIST_ROWS)
+            nc.vector.tensor_copy(dest, table_words[a][:].indirect(which[:, cols]))
+
+        first_plane = {}
+
+        def gather_scales(side, first, count, queue, tag=None):
+            which = tail_list if side == "tail" else head_list
+            cols = slice(first // LIST_ROWS, (first + count) // LIST_ROWS)
+            both = held([P, count], U8, "first_plane_%s%d" % (side, first), tag)
+            nc.vector.tensor_copy(both[:], table_scales[:].indirect(which[:, cols]))
+            queue.dma_start(second_plane[side, first][0:100, :].bitcast(I32), both[4:104, :].bitcast(I32))
+            first_plane[side, first] = both
+
+        def plane_of(side, first, a):
+            return first_plane[side, first] if a == 0 else second_plane[side, first]
+
+        tail_words = {}
+
+        def gather_tail_words(c, tag=None):
+            tail_words[c] = held([P, PASSES * CHUNK], U16, "tail_words%d" % c, tag)
+            for a in range(PASSES):
+                gather_words("tail", a, c * CHUNK, CHUNK, tail_words[c][:, a * CHUNK : (a + 1) * CHUNK])
+
+        head_words = {}
+
+        def gather_head_words(tag):
+            words = held([P, PASSES * S], U16, "head_words", tag)
+            for first in range(0, S, CHUNK):
+                for a in range(PASSES):
+                    gather_words("head", a, first, CHUNK, words[:, a * S + first : a * S + first + CHUNK])
+            for col in range(0, S, STRIP):
+                for a in range(PASSES):
+                    head_words[col // STRIP, a] = words[:, a * S + col : a * S + col + STRIP]
+
+        gather_scales("tail", 0, CHUNK, nc.scalar)
+        gather_tail_words(0)
+
+        codes = {"im": held([P, PASSES * H], I32, "wi_codes"), "re": held([P, PASSES * H], I32, "wr_codes")}
+        scales = {"im": held([P, PASSES * H], U8, "wi_plane"), "re": held([P, PASSES * H], U8, "wr_plane")}
+        nc.vector.tensor_copy(
+            codes["im"][:].rearrange("p (a t g m) -> p a g t m", a=PASSES, t=PACK, m=4),
+            wi_raw[:].rearrange("p (a g m t) -> p a g t m", a=PASSES, t=PACK, m=4),
+        )
+        nc.vector.tensor_copy(
+            scales["im"][:].rearrange("p (a t g m) -> p a g t m", a=PASSES, t=PACK, m=16),
+            wi_scales_raw[:].rearrange("p (a g m t) -> p a g t m", a=PASSES, t=PACK, m=16),
+        )
+
+        wr_rounded = [held([P, PACK * H], BF16, "wr_rounded%d" % a) for a in range(PASSES)]
+        for a in range(PASSES):
+            nc.scalar.copy(
+                wr_rounded[a][:].rearrange("p (t m j) -> p m j t", t=PACK, j=PACK),
+                wr_raw[a][:].rearrange("p j (m t) -> p m j t", t=PACK),
+            )
+
+        gain_cols = held([P, PACK], F32, "gain_cols", "wr_raw0")
+        nc.sync.dma_start(gain_cols[:], gain.rearrange("(p t) -> p t", t=PACK))
+
+        def weight(part, a, t):
+            cols = slice(a * H + t * P, a * H + (t + 1) * P)
+            return codes[part][:, cols].bitcast(FP8X4), scales[part][:, cols]
+
+        tails = {}
+        tail_banks = {}
+
+        def tail_products(part, c):
+            banks = [psum.tile([P, CHUNK], F32, name="bank", tag="bank") for t in range(PACK)]
+            for a in range(PASSES):
+                for t in range(PACK):
+                    w, w_scale = weight(part, a, t)
+                    nc.tensor.matmul_mx(
+                        out=banks[t][:],
+                        lhsT=w,
+                        lhsT_scale=w_scale,
+                        rhs=tail_words[c][:, a * CHUNK : (a + 1) * CHUNK].bitcast(FP4X4),
+                        rhs_scale=plane_of("tail", c * CHUNK, a)[:],
+                        start=(a == 0),
+                        stop=(a == PASSES - 1),
+                    )
+            tail_banks[part, c] = banks
+
+        def tail_copies(part, c, tag=None):
+            banks = tail_banks[part, c]
+            tails[part, c] = held([P, PACK, CHUNK], F32, "tail_%s%d" % (part, c), tag)
+            for t in range(PACK):
+                nc.scalar.activation(tails[part, c][:, t, :], banks[t][:], COPY, scale=gain_cols[:, t : t + 1])
+
+        def quantise_wr(a):
+            cols = slice(a * H, (a + 1) * H)
+            nc.vector.quantize_mx(out=codes["re"][:, cols].bitcast(FP8X4), scales=scales["re"][:, cols], in_=wr_rounded[a][:])
+
+        products = {}
+
+        def head_products(s):
+            c, within = divmod(s * STRIP, CHUNK)
+            for part in ("im", "re"):
+                bank = psum.tile([P, PACK, STRIP], F32, name="bank", tag="bank")
+                for t in range(PACK):
+                    for a in range(PASSES):
+                        w, w_scale = weight(part, a, t)
+                        nc.tensor.matmul_mx(
+                            out=bank[:, t, :],
+                            lhsT=w,
+                            lhsT_scale=w_scale,
+                            rhs=head_words[s, a].bitcast(FP4X4),
+                            rhs_scale=plane_of("head", 0, a)[:, s * STRIP : (s + 1) * STRIP],
+                            start=(a == 0),
+                            stop=(a == PASSES - 1),
+                        )
+                products[part, s] = held([P, PACK, STRIP], F32, "product_%s%d" % (part, s))
+                nc.vector.tensor_tensor(
+                    products[part, s][:], bank[:], tails[part, c][:, :, within : within + STRIP], MULT
+                )
+
+        h_rounded = {}
+
+        def add_products(s, engine):
+            for first, count in SCORE_GROUPS:
+                if first <= s * STRIP < first + count:
+                    if first not in h_rounded:
+                        h_rounded[first] = held([P, PACK * count], BF16, "h_rounded%d" % first)
+                    at = PACK * (s * STRIP - first)
+                    engine.tensor_tensor(
+                        h_rounded[first][:, at : at + PACK * STRIP].rearrange("p (g i t) -> p g t i", i=4, t=PACK),
+                        products["im", s][:].rearrange("p t (g i) -> p g t i", i=4),
+                        products["re", s][:].rearrange("p t (g i) -> p g t i", i=4),
+                        ADD,
+                    )
+
+        def scores(first, count):
+            h_codes = held([P, count], I32, "h_codes%d" % first)
+            h_plane = held([P, count], U8, "h_plane%d" % first)
+            nc.vector.quantize_mx(out=h_codes[:].bitcast(FP8X4), scales=h_plane[:], in_=h_rounded[first][:])
+            per_bank = min(CHUNK // count, 2)
+            last = first + count == S
+            for n0 in range(0, N // P, per_bank):
+                bank = psum.tile([P, per_bank, count], F32, name="bank", tag="bank")
+                for n in range(n0, n0 + per_bank):
+                    nc.tensor.matmul_mx(
+                        out=bank[:, n - n0, :],
+                        lhsT=wrel_codes[:, 2 * P * n : 2 * P * (n + 1)].bitcast(FP4X4),
+                        lhsT_scale=wrel_plane[:, P * n : P * (n + 1)],
+                        rhs=h_codes[:].bitcast(FP8X4),
+                        rhs_scale=h_plane[:],
+                        start=True,
+                        stop=True,
+                    )
+                if n0 % 2 == 0:
+                    result = held([P, 2, count], F32, "result%d_%d" % (first, n0))
+                for n in range(n0, n0 + per_bank):
+                    if last and n0 > 0:
+                        nc.vector.tensor_scalar(result[:, n % 2, :], bank[:, n - n0, :], bias_cols[:, n : n + 1], None, ADD)
+                    else:
+                        nc.scalar.activation(
+                            result[:, n % 2, :], bank[:, n - n0, :], IDENTITY, bias=bias_cols[:, n : n + 1]
+                        )
+                if (n0 + per_bank) % 2 == 0:
+                    rows = slice((n0 // 2) * 2 * P, (n0 // 2 + 1) * 2 * P)
+                    nc.sync.dma_start(out[rows, first : first + count].rearrange("(n p) j -> p n j", p=P), result[:])
+
+        tail_products("im", 0)
+        gather_scales("tail", CHUNK, CHUNK, nc.sync, "wi_scales_raw")
+        gather_tail_words(1, "wi_raw")
+        tail_products("im", 1)
+        tail_copies("im", 0, "wr_raw1")
+        quantise_wr(0)
+        gather_scales("head", 0, S, nc.sync, "wr_rounded0")
+        quantise_wr(1)
+        tail_products("re", 0)
+        gather_head_words("wr_rounded1")
+        wrel_codes = held([P, 2 * N], U8, "wrel_codes", "table_words0")
+        nc.sync.dma_start(wrel_codes[:].bitcast(I32), wrel_words[0].bitcast(I32))
+        wrel_plane = held([P, N], U8, "wrel_plane", "table_scales")
+        nc.gpsimd.memset(wrel_plane[:].bitcast(I32), 0)
+        for q in range(4):
+            nc.sync.dma_start(
+                wrel_plane[32 * q : 32 * q + 4, :].bitcast(I32), wrel_scales[0, 4 * q : 4 * q + 4, :].bitcast(I32)
+            )
+        bias_cols = held([P, N // P], F32, "bias_cols", "table_words1")
+        with nc.allow_non_contiguous_dma(reason="one bias value for each output row"):
+            nc.sync.dma_start(bias_cols[:], bias.rearrange("(n p) -> p n", p=P))
+
+        tail_copies("re", 0)
+        tail_products("re", 1)
+        tail_copies("im", 1)
+        tail_copies("re", 1)
+
+        for s in range(6):
+            head_products(s)
+            if s == 5:
+                scores(0, 512)
+            add_products(s, nc.vector if s == 3 else nc.gpsimd)
+        head_products(6)
+        head_products(7)
+        scores(512, 256)
+        add_products(6, nc.vector)
+        scores(768, 128)
+        add_products(7, nc.vector)
+        scores(896, 128)

@@ -34,7 +34,7 @@ def tile_list_complex_kinship_scores_kernel(
     with ExitStack() as ctx:
         lists = ctx.enter_context(tc.tile_pool(name="lists", bufs=1))
         keep = ctx.enter_context(tc.tile_pool(name="keep", bufs=1))
-        psum = ctx.enter_context(tc.psum_pool(name="psum", bufs=8))
+        psum = ctx.enter_context(tc.psum_pool(name="psum", bufs=1))
 
         def held(shape, dtype, name, tag=None):
             return keep.tile(shape, dtype, name=name, tag=tag or name, align_bytes=ALIGN)
@@ -44,19 +44,14 @@ def tile_list_complex_kinship_scores_kernel(
 
         table_scales = held([P, T], U8, "table_scales")
         wi_scales_raw = held([P, PASSES * H], U8, "wi_scales_raw")
-        second_plane = {}
-        for side, first, count in (("tail", 0, CHUNK), ("tail", CHUNK, CHUNK), ("head", 0, S)):
-            second_plane[side, first] = held([P, count], U8, "second_plane_%s%d" % (side, first))
-        nc.gpsimd.memset(table_scales[:].bitcast(I32), 0)
         nc.gpsimd.memset(wi_scales_raw[:].bitcast(I32), 0)
-        for key in second_plane:
-            nc.gpsimd.memset(second_plane[key][96:P, :].bitcast(I32), 0)
+        for rows, engine in ((slice(0, 16), nc.gpsimd), (slice(32, 48), nc.gpsimd), (slice(64, P), nc.vector)):
+            engine.memset(table_scales[rows, :].bitcast(I32), 0)
 
         nc.sync.dma_start(tail_list[:], offs2)
-        for q in range(4):
-            nc.sync.dma_start(
-                table_scales[32 * q : 32 * q + 8, :].bitcast(I32), tab_scales[:, 4 * q : 4 * q + 4, :].bitcast(I32)
-            )
+        scale_rows = tab_scales.bitcast(I32).rearrange("a (h q r) c -> q (a h) r c", h=2, q=2)
+        for q in range(2):
+            nc.sync.dma_start(table_scales[32 * q + 16 : 32 * q + 32, :].bitcast(I32), scale_rows[q])
         table_words = [held([P, T], U16, "table_words%d" % a) for a in range(PASSES)]
         for a in range(PASSES):
             nc.sync.dma_start(table_words[a][:].bitcast(I32), tab_words[a].bitcast(I32))
@@ -66,32 +61,40 @@ def tile_list_complex_kinship_scores_kernel(
             wi_words.rearrange("a p c i -> p a (c i)").bitcast(I32),
         )
         for q in range(4):
-            nc.gpsimd.dma_start(
+            nc.scalar.dma_start(
                 wi_scales_raw[32 * q : 32 * q + 4, :].bitcast(I32).rearrange("r (a c) -> r a c", a=PASSES),
                 wi_scales[:, 4 * q : 4 * q + 4, :].bitcast(I32).rearrange("a r c -> r a c"),
             )
-        wr_raw = [held([P, PACK, H], F32, "wr_raw%d" % a) for a in range(PASSES)]
-        for a in range(PASSES):
+        wr_raw = {}
+
+        def load_wr(a, tag):
+            wr_raw[a] = held([P, PACK, H], F32, "wr_raw%d" % a, tag)
             nc.sync.dma_start(wr_raw[a][:], wr[512 * a : 512 * (a + 1), :].rearrange("(p j) c -> p j c", j=PACK))
+
+        load_wr(0, "wr_raw0")
         nc.sync.dma_start(head_list[:], offs)
+        gain_cols = held([P, PACK], F32, "gain_cols")
+        nc.sync.dma_start(gain_cols[:], gain.rearrange("(p t) -> p t", t=PACK))
 
         def gather_words(side, a, first, count, dest):
             which = tail_list if side == "tail" else head_list
             cols = slice(first // LIST_ROWS, (first + count) // LIST_ROWS)
             nc.vector.tensor_copy(dest, table_words[a][:].indirect(which[:, cols]))
 
-        first_plane = {}
+        planes = {}
 
-        def gather_scales(side, first, count, queue, tag=None):
+        def gather_scales(side, queue, tag=None):
             which = tail_list if side == "tail" else head_list
-            cols = slice(first // LIST_ROWS, (first + count) // LIST_ROWS)
-            both = held([P, count], U8, "first_plane_%s%d" % (side, first), tag)
-            nc.vector.tensor_copy(both[:], table_scales[:].indirect(which[:, cols]))
-            queue.dma_start(second_plane[side, first][0:100, :].bitcast(I32), both[4:104, :].bitcast(I32))
-            first_plane[side, first] = both
-
-        def plane_of(side, first, a):
-            return first_plane[side, first] if a == 0 else second_plane[side, first]
+            picked = held([P, S], U8, "picked_scales_%s" % side, tag)
+            nc.vector.tensor_copy(picked[:], table_scales[:].indirect(which[:]))
+            for a in range(PASSES):
+                planes[side, a] = held([P, S], U8, "plane_%s%d" % (side, a))
+                for h in range(2):
+                    source = 16 + 8 * a + 4 * h
+                    queue.dma_start(
+                        planes[side, a][64 * h : 64 * h + 64, :].bitcast(I32),
+                        picked[source : source + 64, :].bitcast(I32),
+                    )
 
         tail_words = {}
 
@@ -111,29 +114,27 @@ def tile_list_complex_kinship_scores_kernel(
                 for a in range(PASSES):
                     head_words[col // STRIP, a] = words[:, a * S + col : a * S + col + STRIP]
 
-        gather_scales("tail", 0, CHUNK, nc.scalar)
+        gather_scales("tail", nc.scalar)
         gather_tail_words(0)
 
         codes = {"im": held([P, PASSES * H], I32, "wi_codes"), "re": held([P, PASSES * H], I32, "wr_codes")}
         scales = {"im": held([P, PASSES * H], U8, "wi_plane"), "re": held([P, PASSES * H], U8, "wr_plane")}
-        nc.vector.tensor_copy(
-            codes["im"][:].rearrange("p (a t g m) -> p a g t m", a=PASSES, t=PACK, m=4),
-            wi_raw[:].rearrange("p (a g m t) -> p a g t m", a=PASSES, t=PACK, m=4),
-        )
-        nc.vector.tensor_copy(
+        nc.gpsimd.tensor_copy(
             scales["im"][:].rearrange("p (a t g m) -> p a g t m", a=PASSES, t=PACK, m=16),
             wi_scales_raw[:].rearrange("p (a g m t) -> p a g t m", a=PASSES, t=PACK, m=16),
         )
 
+        nc.gpsimd.tensor_copy(
+            codes["im"][:].rearrange("p (a t g m) -> p a g t m", a=PASSES, t=PACK, m=4),
+            wi_raw[:].rearrange("p (a g m t) -> p a g t m", a=PASSES, t=PACK, m=4),
+        )
+        load_wr(1, "wi_scales_raw")
         wr_rounded = [held([P, PACK * H], BF16, "wr_rounded%d" % a) for a in range(PASSES)]
         for a in range(PASSES):
             nc.scalar.copy(
                 wr_rounded[a][:].rearrange("p (t m j) -> p m j t", t=PACK, j=PACK),
                 wr_raw[a][:].rearrange("p j (m t) -> p m j t", t=PACK),
             )
-
-        gain_cols = held([P, PACK], F32, "gain_cols", "wr_raw0")
-        nc.sync.dma_start(gain_cols[:], gain.rearrange("(p t) -> p t", t=PACK))
 
         def weight(part, a, t):
             cols = slice(a * H + t * P, a * H + (t + 1) * P)
@@ -143,16 +144,16 @@ def tile_list_complex_kinship_scores_kernel(
         tail_banks = {}
 
         def tail_products(part, c):
-            banks = [psum.tile([P, CHUNK], F32, name="bank", tag="bank") for t in range(PACK)]
-            for a in range(PASSES):
-                for t in range(PACK):
+            banks = [psum.tile([P, CHUNK], F32, name="bank", tag="bank%d" % (PACK * c + t)) for t in range(PACK)]
+            for t in range(PACK):
+                for a in range(PASSES):
                     w, w_scale = weight(part, a, t)
                     nc.tensor.matmul_mx(
                         out=banks[t][:],
                         lhsT=w,
                         lhsT_scale=w_scale,
                         rhs=tail_words[c][:, a * CHUNK : (a + 1) * CHUNK].bitcast(FP4X4),
-                        rhs_scale=plane_of("tail", c * CHUNK, a)[:],
+                        rhs_scale=planes["tail", a][:, c * CHUNK : (c + 1) * CHUNK],
                         start=(a == 0),
                         stop=(a == PASSES - 1),
                     )
@@ -172,8 +173,8 @@ def tile_list_complex_kinship_scores_kernel(
 
         def head_products(s):
             c, within = divmod(s * STRIP, CHUNK)
-            for part in ("im", "re"):
-                bank = psum.tile([P, PACK, STRIP], F32, name="bank", tag="bank")
+            for half, part in enumerate(("im", "re")):
+                bank = psum.tile([P, PACK, STRIP], F32, name="bank", tag="bank%d" % (2 * (s % 2) + half))
                 for t in range(PACK):
                     for a in range(PASSES):
                         w, w_scale = weight(part, a, t)
@@ -182,13 +183,16 @@ def tile_list_complex_kinship_scores_kernel(
                             lhsT=w,
                             lhsT_scale=w_scale,
                             rhs=head_words[s, a].bitcast(FP4X4),
-                            rhs_scale=plane_of("head", 0, a)[:, s * STRIP : (s + 1) * STRIP],
+                            rhs_scale=planes["head", a][:, s * STRIP : (s + 1) * STRIP],
                             start=(a == 0),
                             stop=(a == PASSES - 1),
                         )
-                products[part, s] = held([P, PACK, STRIP], F32, "product_%s%d" % (part, s))
+                products[part, s] = held([P, PACK * STRIP], F32, "product_%s%d" % (part, s))
                 nc.vector.tensor_tensor(
-                    products[part, s][:], bank[:], tails[part, c][:, :, within : within + STRIP], MULT
+                    products[part, s][:].rearrange("p (u j e) -> p u j e", u=2, e=2),
+                    bank[:].rearrange("p (u e) j -> p u j e", e=2),
+                    tails[part, c][:, :, within : within + STRIP].rearrange("p (u e) j -> p u j e", e=2),
+                    MULT,
                 )
 
         h_rounded = {}
@@ -200,20 +204,20 @@ def tile_list_complex_kinship_scores_kernel(
                         h_rounded[first] = held([P, PACK * count], BF16, "h_rounded%d" % first)
                     at = PACK * (s * STRIP - first)
                     engine.tensor_tensor(
-                        h_rounded[first][:, at : at + PACK * STRIP].rearrange("p (g i t) -> p g t i", i=4, t=PACK),
-                        products["im", s][:].rearrange("p t (g i) -> p g t i", i=4),
-                        products["re", s][:].rearrange("p t (g i) -> p g t i", i=4),
+                        h_rounded[first][:, at : at + PACK * STRIP].rearrange("p (j u e) -> p j u e", u=2, e=2),
+                        products["im", s][:].rearrange("p (u j e) -> p j u e", u=2, e=2),
+                        products["re", s][:].rearrange("p (u j e) -> p j u e", u=2, e=2),
                         ADD,
                     )
 
-        def scores(first, count):
+        def scores(first, count, first_bank):
             h_codes = held([P, count], I32, "h_codes%d" % first)
             h_plane = held([P, count], U8, "h_plane%d" % first)
             nc.vector.quantize_mx(out=h_codes[:].bitcast(FP8X4), scales=h_plane[:], in_=h_rounded[first][:])
             per_bank = min(CHUNK // count, 2)
             last = first + count == S
             for n0 in range(0, N // P, per_bank):
-                bank = psum.tile([P, per_bank, count], F32, name="bank", tag="bank")
+                bank = psum.tile([P, per_bank, count], F32, name="bank", tag="bank%d" % (first_bank + n0 // per_bank))
                 for n in range(n0, n0 + per_bank):
                     nc.tensor.matmul_mx(
                         out=bank[:, n - n0, :],
@@ -238,12 +242,11 @@ def tile_list_complex_kinship_scores_kernel(
                     nc.sync.dma_start(out[rows, first : first + count].rearrange("(n p) j -> p n j", p=P), result[:])
 
         tail_products("im", 0)
-        gather_scales("tail", CHUNK, CHUNK, nc.sync, "wi_scales_raw")
-        gather_tail_words(1, "wi_raw")
+        gather_tail_words(1)
         tail_products("im", 1)
-        tail_copies("im", 0, "wr_raw1")
+        tail_copies("im", 0, "wi_scales_raw")
         quantise_wr(0)
-        gather_scales("head", 0, S, nc.sync, "wr_rounded0")
+        gather_scales("head", nc.sync, "wr_rounded0")
         quantise_wr(1)
         tail_products("re", 0)
         gather_head_words("wr_rounded1")
@@ -260,19 +263,17 @@ def tile_list_complex_kinship_scores_kernel(
             nc.sync.dma_start(bias_cols[:], bias.rearrange("(n p) -> p n", p=P))
 
         tail_copies("re", 0)
-        tail_products("re", 1)
-        tail_copies("im", 1)
-        tail_copies("re", 1)
-
-        for s in range(6):
+        for s in range(S // STRIP):
+            if s == 2:
+                tail_copies("im", 1)
+                tail_products("re", 1)
+                tail_copies("re", 1)
+            if s == 7:
+                scores(512, 256, 4)
             head_products(s)
             if s == 5:
-                scores(0, 512)
-            add_products(s, nc.vector if s == 3 else nc.gpsimd)
-        head_products(6)
-        head_products(7)
-        scores(512, 256)
-        add_products(6, nc.vector)
-        scores(768, 128)
-        add_products(7, nc.vector)
-        scores(896, 128)
+                scores(0, 512, 4)
+            if s == 7:
+                scores(768, 128, 6)
+            add_products(s, nc.vector if s == 7 else nc.gpsimd)
+        scores(896, 128, 4)

@@ -24,7 +24,7 @@ CHUNK = 512
 STRIP = 128
 LIST_ROWS = 16
 ALIGN = 64
-SCORE_GROUPS = ((0, 512), (512, 256), (768, 128), (896, 128))
+SCORE_GROUPS = ((0, 256), (256, 256), (512, 256), (768, 128), (896, 128))
 
 
 def tile_list_complex_kinship_scores_kernel(
@@ -47,34 +47,31 @@ def tile_list_complex_kinship_scores_kernel(
         nc.gpsimd.memset(wi_scales_raw[:].bitcast(I32), 0)
         for rows, engine in ((slice(0, 16), nc.gpsimd), (slice(32, 48), nc.gpsimd), (slice(64, P), nc.vector)):
             engine.memset(table_scales[rows, :].bitcast(I32), 0)
+        wrel_plane = held([P, N], U8, "wrel_plane")
+        nc.gpsimd.memset(wrel_plane[:].bitcast(I32), 0)
 
         nc.sync.dma_start(tail_list[:], offs2)
         scale_rows = tab_scales.bitcast(I32).rearrange("a (h q r) c -> q (a h) r c", h=2, q=2)
         for q in range(2):
             nc.sync.dma_start(table_scales[32 * q + 16 : 32 * q + 32, :].bitcast(I32), scale_rows[q])
         table_words = [held([P, T], U16, "table_words%d" % a) for a in range(PASSES)]
-        for a in range(PASSES):
-            nc.sync.dma_start(table_words[a][:].bitcast(I32), tab_words[a].bitcast(I32))
         wi_raw = held([P, PASSES * H], I32, "wi_raw")
+        nc.sync.dma_start(table_words[0][:].bitcast(I32), tab_words[0].bitcast(I32))
+        for q in range(4):
+            nc.sync.dma_start(
+                wi_scales_raw[32 * q : 32 * q + 4, :].bitcast(I32).rearrange("r (a c) -> r a c", a=PASSES),
+                wi_scales[:, 4 * q : 4 * q + 4, :].bitcast(I32).rearrange("a r c -> r a c"),
+            )
         nc.sync.dma_start(
             wi_raw[:].rearrange("p (a c) -> p a c", a=PASSES),
             wi_words.rearrange("a p c i -> p a (c i)").bitcast(I32),
         )
-        for q in range(4):
-            nc.scalar.dma_start(
-                wi_scales_raw[32 * q : 32 * q + 4, :].bitcast(I32).rearrange("r (a c) -> r a c", a=PASSES),
-                wi_scales[:, 4 * q : 4 * q + 4, :].bitcast(I32).rearrange("a r c -> r a c"),
-            )
-        wr_raw = {}
-
-        def load_wr(a, tag):
-            wr_raw[a] = held([P, PACK, H], F32, "wr_raw%d" % a, tag)
-            nc.sync.dma_start(wr_raw[a][:], wr[512 * a : 512 * (a + 1), :].rearrange("(p j) c -> p j c", j=PACK))
-
-        load_wr(0, "wr_raw0")
+        nc.sync.dma_start(table_words[1][:].bitcast(I32), tab_words[1].bitcast(I32))
         nc.sync.dma_start(head_list[:], offs)
-        gain_cols = held([P, PACK], F32, "gain_cols")
-        nc.sync.dma_start(gain_cols[:], gain.rearrange("(p t) -> p t", t=PACK))
+        wr_raw = [held([P, PACK, H], F32, "wr_raw%d" % a) for a in range(PASSES)]
+
+        def load_wr(a):
+            nc.sync.dma_start(wr_raw[a][:], wr[512 * a : 512 * (a + 1), :].rearrange("(p j) c -> p j c", j=PACK))
 
         def gather_words(side, a, first, count, dest):
             which = tail_list if side == "tail" else head_list
@@ -82,39 +79,45 @@ def tile_list_complex_kinship_scores_kernel(
             nc.vector.tensor_copy(dest, table_words[a][:].indirect(which[:, cols]))
 
         planes = {}
+        picked = {}
 
-        def gather_scales(side, queue, tag=None):
+        def gather_scales(side, first, count, tag=None):
             which = tail_list if side == "tail" else head_list
-            picked = held([P, S], U8, "picked_scales_%s" % side, tag)
-            nc.vector.tensor_copy(picked[:], table_scales[:].indirect(which[:]))
-            for a in range(PASSES):
-                planes[side, a] = held([P, S], U8, "plane_%s%d" % (side, a))
-                for h in range(2):
-                    source = 16 + 8 * a + 4 * h
-                    queue.dma_start(
-                        planes[side, a][64 * h : 64 * h + 64, :].bitcast(I32),
-                        picked[source : source + 64, :].bitcast(I32),
-                    )
+            picked[side, first] = held([P, count], U8, "picked_scales_%s%d" % (side, first), tag)
+            cols = slice(first // LIST_ROWS, (first + count) // LIST_ROWS)
+            nc.vector.tensor_copy(picked[side, first][:], table_scales[:].indirect(which[:, cols]))
+
+        def place_scales(side, first, count, a):
+            planes[side, first, a] = held([P, count], U8, "plane_%s%d_%d" % (side, first, a))
+            for h in range(2):
+                source = 16 + 8 * a + 4 * h
+                nc.sync.dma_start(
+                    planes[side, first, a][64 * h : 64 * h + 64, :].bitcast(I32),
+                    picked[side, first][source : source + 64, :].bitcast(I32),
+                )
 
         tail_words = {}
 
         def gather_tail_words(c, tag=None):
-            tail_words[c] = held([P, PASSES * CHUNK], U16, "tail_words%d" % c, tag)
             for a in range(PASSES):
-                gather_words("tail", a, c * CHUNK, CHUNK, tail_words[c][:, a * CHUNK : (a + 1) * CHUNK])
+                tail_words[c, a] = held([P, CHUNK], U16, "tail_words%d_%d" % (c, a), tag if a == 0 else None)
+                gather_words("tail", a, c * CHUNK, CHUNK, tail_words[c, a][:])
 
         head_words = {}
 
-        def gather_head_words(tag):
-            words = held([P, PASSES * S], U16, "head_words", tag)
-            for first in range(0, S, CHUNK):
-                for a in range(PASSES):
-                    gather_words("head", a, first, CHUNK, words[:, a * S + first : a * S + first + CHUNK])
-            for col in range(0, S, STRIP):
-                for a in range(PASSES):
-                    head_words[col // STRIP, a] = words[:, a * S + col : a * S + col + STRIP]
+        def gather_head_words(pieces, tag):
+            words = held([P, len(pieces) * CHUNK], U16, "head_words_" + tag, tag)
+            for i, (c, a) in enumerate(pieces):
+                head_words[c, a] = words[:, i * CHUNK : (i + 1) * CHUNK]
+                gather_words("head", a, c * CHUNK, CHUNK, head_words[c, a])
 
-        gather_scales("tail", nc.scalar)
+        gather_scales("tail", 0, S)
+        load_wr(0)
+        for a in range(PASSES):
+            place_scales("tail", 0, S, a)
+        load_wr(1)
+        gain_cols = held([P, PACK], F32, "gain_cols")
+        nc.sync.dma_start(gain_cols[:], gain.rearrange("(p t) -> p t", t=PACK))
         gather_tail_words(0)
 
         codes = {"im": held([P, PASSES * H], I32, "wi_codes"), "re": held([P, PASSES * H], I32, "wr_codes")}
@@ -124,17 +127,19 @@ def tile_list_complex_kinship_scores_kernel(
             wi_scales_raw[:].rearrange("p (a g m t) -> p a g t m", a=PASSES, t=PACK, m=16),
         )
 
-        nc.gpsimd.tensor_copy(
-            codes["im"][:].rearrange("p (a t g m) -> p a g t m", a=PASSES, t=PACK, m=4),
-            wi_raw[:].rearrange("p (a g m t) -> p a g t m", a=PASSES, t=PACK, m=4),
-        )
-        load_wr(1, "wi_scales_raw")
+        for a in range(PASSES):
+            nc.gpsimd.tensor_copy(
+                codes["im"][:, a * H : (a + 1) * H].rearrange("p (t g m) -> p g t m", t=PACK, m=4),
+                wi_raw[:, a * H : (a + 1) * H].rearrange("p (g m t) -> p g t m", t=PACK, m=4),
+            )
         wr_rounded = [held([P, PACK * H], BF16, "wr_rounded%d" % a) for a in range(PASSES)]
         for a in range(PASSES):
+            rounded = wr_rounded[a][:].rearrange("p (t m j) -> p t m j", t=PACK, j=PACK)
+            raw = wr_raw[a][:].rearrange("p j (m t) -> p t m j", t=PACK)
             nc.scalar.copy(
-                wr_rounded[a][:].rearrange("p (t m j) -> p m j t", t=PACK, j=PACK),
-                wr_raw[a][:].rearrange("p j (m t) -> p m j t", t=PACK),
+                rounded[:, 0:3, :, :].rearrange("p t m j -> p m j t"), raw[:, 0:3, :, :].rearrange("p t m j -> p m j t")
             )
+            nc.gpsimd.tensor_copy(rounded[:, 3, :, :], raw[:, 3, :, :])
 
         def weight(part, a, t):
             cols = slice(a * H + t * P, a * H + (t + 1) * P)
@@ -145,15 +150,16 @@ def tile_list_complex_kinship_scores_kernel(
 
         def tail_products(part, c):
             banks = [psum.tile([P, CHUNK], F32, name="bank", tag="bank%d" % (PACK * c + t)) for t in range(PACK)]
-            for t in range(PACK):
-                for a in range(PASSES):
+            steps = [(t, a) for t in range(PACK) for a in range(PASSES)]
+            for t, a in steps:
+                if True:
                     w, w_scale = weight(part, a, t)
                     nc.tensor.matmul_mx(
                         out=banks[t][:],
                         lhsT=w,
                         lhsT_scale=w_scale,
-                        rhs=tail_words[c][:, a * CHUNK : (a + 1) * CHUNK].bitcast(FP4X4),
-                        rhs_scale=planes["tail", a][:, c * CHUNK : (c + 1) * CHUNK],
+                        rhs=tail_words[c, a][:].bitcast(FP4X4),
+                        rhs_scale=planes["tail", 0, a][:, c * CHUNK : (c + 1) * CHUNK],
                         start=(a == 0),
                         stop=(a == PASSES - 1),
                     )
@@ -161,7 +167,9 @@ def tile_list_complex_kinship_scores_kernel(
 
         def tail_copies(part, c, tag=None):
             banks = tail_banks[part, c]
-            tails[part, c] = held([P, PACK, CHUNK], F32, "tail_%s%d" % (part, c), tag)
+            if c == 0:
+                tails[part] = held([P, 2 * PACK, CHUNK], F32, "tail_%s" % part, tag)
+            tails[part, c] = tails[part][:, PACK * c : PACK * (c + 1), :]
             for t in range(PACK):
                 nc.scalar.activation(tails[part, c][:, t, :], banks[t][:], COPY, scale=gain_cols[:, t : t + 1])
 
@@ -182,8 +190,8 @@ def tile_list_complex_kinship_scores_kernel(
                             out=bank[:, t, :],
                             lhsT=w,
                             lhsT_scale=w_scale,
-                            rhs=head_words[s, a].bitcast(FP4X4),
-                            rhs_scale=planes["head", a][:, s * STRIP : (s + 1) * STRIP],
+                            rhs=head_words[c, a][:, within : within + STRIP].bitcast(FP4X4),
+                            rhs_scale=planes["head", 0, a][:, s * STRIP : (s + 1) * STRIP],
                             start=(a == 0),
                             stop=(a == PASSES - 1),
                         )
@@ -242,38 +250,42 @@ def tile_list_complex_kinship_scores_kernel(
                     nc.sync.dma_start(out[rows, first : first + count].rearrange("(n p) j -> p n j", p=P), result[:])
 
         tail_products("im", 0)
-        gather_tail_words(1)
+        gather_tail_words(1, "wi_raw")
         tail_products("im", 1)
-        tail_copies("im", 0, "wi_scales_raw")
+        tail_copies("im", 0, "wr_raw1")
+        gather_scales("head", 0, S, "wi_scales_raw")
+        for a in range(PASSES):
+            place_scales("head", 0, S, a)
         quantise_wr(0)
-        gather_scales("head", nc.sync, "wr_rounded0")
         quantise_wr(1)
         tail_products("re", 0)
-        gather_head_words("wr_rounded1")
-        wrel_codes = held([P, 2 * N], U8, "wrel_codes", "table_words0")
-        nc.sync.dma_start(wrel_codes[:].bitcast(I32), wrel_words[0].bitcast(I32))
-        wrel_plane = held([P, N], U8, "wrel_plane", "table_scales")
-        nc.gpsimd.memset(wrel_plane[:].bitcast(I32), 0)
-        for q in range(4):
-            nc.sync.dma_start(
-                wrel_plane[32 * q : 32 * q + 4, :].bitcast(I32), wrel_scales[0, 4 * q : 4 * q + 4, :].bitcast(I32)
-            )
-        bias_cols = held([P, N // P], F32, "bias_cols", "table_words1")
-        with nc.allow_non_contiguous_dma(reason="one bias value for each output row"):
-            nc.sync.dma_start(bias_cols[:], bias.rearrange("(n p) -> p n", p=P))
-
+        gather_head_words([(0, 0), (0, 1), (1, 0)], "wr_rounded1")
         tail_copies("re", 0)
+        tail_copies("im", 1)
         for s in range(S // STRIP):
-            if s == 2:
-                tail_copies("im", 1)
+            if s == 4:
                 tail_products("re", 1)
                 tail_copies("re", 1)
+            if s == 3:
+                gather_head_words([(1, 1)], "product_im1")
+                wrel_codes = held([P, 2 * N], U8, "wrel_codes")
+                nc.sync.dma_start(wrel_codes[:].bitcast(I32), wrel_words[0].bitcast(I32))
+                for q in range(4):
+                    nc.sync.dma_start(
+                        wrel_plane[32 * q : 32 * q + 4, :].bitcast(I32), wrel_scales[0, 4 * q : 4 * q + 4, :].bitcast(I32)
+                    )
+                bias_cols = held([P, N // P], F32, "bias_cols")
+                with nc.allow_non_contiguous_dma(reason="one bias value for each output row"):
+                    nc.sync.dma_start(bias_cols[:], bias.rearrange("(n p) -> p n", p=P))
+
             if s == 7:
                 scores(512, 256, 4)
             head_products(s)
+            if s == 4:
+                scores(0, 256, 4)
             if s == 5:
-                scores(0, 512, 4)
+                scores(256, 256, 6)
             if s == 7:
                 scores(768, 128, 6)
             add_products(s, nc.vector if s == 7 else nc.gpsimd)
-        scores(896, 128, 4)
+        scores(896, 128, 0)

@@ -197,9 +197,9 @@ def tile_list_complex_kinship_scores_kernel(
                         )
                 products[part, s] = held([P, PACK * STRIP], F32, "product_%s%d" % (part, s))
                 nc.vector.tensor_tensor(
-                    products[part, s][:].rearrange("p (u j e) -> p u j e", u=2, e=2),
-                    bank[:].rearrange("p (u e) j -> p u j e", e=2),
-                    tails[part, c][:, :, within : within + STRIP].rearrange("p (u e) j -> p u j e", e=2),
+                    products[part, s][:].rearrange("p (g i t) -> p g t i", i=2, t=PACK),
+                    bank[:].rearrange("p t (g i) -> p g t i", i=2),
+                    tails[part, c][:, :, within : within + STRIP].rearrange("p t (g i) -> p g t i", i=2),
                     MULT,
                 )
 
@@ -212,9 +212,9 @@ def tile_list_complex_kinship_scores_kernel(
                         h_rounded[first] = held([P, PACK * count], BF16, "h_rounded%d" % first)
                     at = PACK * (s * STRIP - first)
                     engine.tensor_tensor(
-                        h_rounded[first][:, at : at + PACK * STRIP].rearrange("p (j u e) -> p j u e", u=2, e=2),
-                        products["im", s][:].rearrange("p (u j e) -> p j u e", u=2, e=2),
-                        products["re", s][:].rearrange("p (u j e) -> p j u e", u=2, e=2),
+                        h_rounded[first][:, at : at + PACK * STRIP],
+                        products["im", s][:],
+                        products["re", s][:],
                         ADD,
                     )
 

@@ -22,8 +22,11 @@ PACK = 4
 PASSES = K // (P * PACK)
 CHUNK = 512
 STRIP = 128
+STRIPS = S // STRIP
 LIST_ROWS = 16
 ALIGN = 64
+HEAD_AHEAD = 3
+SCALAR_SHARE = 64
 SCORE_GROUPS = ((0, 256), (256, 256), (512, 256), (768, 128), (896, 128))
 
 
@@ -39,53 +42,58 @@ def tile_list_complex_kinship_scores_kernel(
         def held(shape, dtype, name, tag=None):
             return keep.tile(shape, dtype, name=name, tag=tag or name, align_bytes=ALIGN)
 
-        head_list = lists.tile([P, S // LIST_ROWS], U16, name="head_list")
-        tail_list = lists.tile([P, S // LIST_ROWS], U16, name="tail_list")
+        def bank_tile(shape, number):
+            return psum.tile(shape, F32, name="bank", tag="bank%d" % number)
 
-        table_scales = held([P, T], U8, "table_scales")
+        offsets = {
+            "head": lists.tile([P, S // LIST_ROWS], U16, name="head_list"),
+            "tail": lists.tile([P, S // LIST_ROWS], U16, name="tail_list"),
+        }
+
         wi_scales_raw = held([P, PASSES * H], U8, "wi_scales_raw")
         nc.gpsimd.memset(wi_scales_raw[:].bitcast(I32), 0)
+        table_scales = held([P, T], U8, "table_scales")
         for rows, engine in ((slice(0, 16), nc.gpsimd), (slice(32, 48), nc.gpsimd), (slice(64, P), nc.vector)):
             engine.memset(table_scales[rows, :].bitcast(I32), 0)
         wrel_plane = held([P, N], U8, "wrel_plane")
         nc.gpsimd.memset(wrel_plane[:].bitcast(I32), 0)
 
-        nc.sync.dma_start(tail_list[:], offs2)
+        table_words = [held([P, T], U16, "table_words%d" % a) for a in range(PASSES)]
+        wi_raw = [held([P, H], I32, "wi_raw%d" % a) for a in range(PASSES)]
+        wr_raw = [held([P, PACK, H], F32, "wr_raw%d" % a) for a in range(PASSES)]
+
+        def load_words(a):
+            nc.sync.dma_start(table_words[a][:].bitcast(I32), tab_words[a].bitcast(I32))
+
+        def load_wi(a):
+            nc.sync.dma_start(wi_raw[a][:], wi_words[a].rearrange("p c i -> p (c i)").bitcast(I32))
+
+        def load_wr(a):
+            nc.sync.dma_start(wr_raw[a][:], wr[512 * a : 512 * (a + 1), :].rearrange("(p j) c -> p j c", j=PACK))
+
+        nc.sync.dma_start(offsets["tail"][:], offs2)
         scale_rows = tab_scales.bitcast(I32).rearrange("a (h q r) c -> q (a h) r c", h=2, q=2)
         for q in range(2):
             nc.sync.dma_start(table_scales[32 * q + 16 : 32 * q + 32, :].bitcast(I32), scale_rows[q])
-        table_words = [held([P, T], U16, "table_words%d" % a) for a in range(PASSES)]
-        wi_raw = held([P, PASSES * H], I32, "wi_raw")
-        nc.sync.dma_start(table_words[0][:].bitcast(I32), tab_words[0].bitcast(I32))
+        load_words(0)
+        load_wi(0)
         for q in range(4):
             nc.sync.dma_start(
                 wi_scales_raw[32 * q : 32 * q + 4, :].bitcast(I32).rearrange("r (a c) -> r a c", a=PASSES),
                 wi_scales[:, 4 * q : 4 * q + 4, :].bitcast(I32).rearrange("a r c -> r a c"),
             )
-        nc.sync.dma_start(
-            wi_raw[:].rearrange("p (a c) -> p a c", a=PASSES),
-            wi_words.rearrange("a p c i -> p a (c i)").bitcast(I32),
-        )
-        nc.sync.dma_start(table_words[1][:].bitcast(I32), tab_words[1].bitcast(I32))
-        nc.sync.dma_start(head_list[:], offs)
-        wr_raw = [held([P, PACK, H], F32, "wr_raw%d" % a) for a in range(PASSES)]
+        load_words(1)
+        load_wi(1)
 
-        def load_wr(a):
-            nc.sync.dma_start(wr_raw[a][:], wr[512 * a : 512 * (a + 1), :].rearrange("(p j) c -> p j c", j=PACK))
-
-        def gather_words(side, a, first, count, dest):
-            which = tail_list if side == "tail" else head_list
-            cols = slice(first // LIST_ROWS, (first + count) // LIST_ROWS)
-            nc.vector.tensor_copy(dest, table_words[a][:].indirect(which[:, cols]))
-
-        planes = {}
         picked = {}
+        words = {}
 
         def gather_scales(side, first, count, tag=None):
-            which = tail_list if side == "tail" else head_list
-            picked[side, first] = held([P, count], U8, "picked_scales_%s%d" % (side, first), tag)
+            picked[side, first] = held([P, count], U8, "picked_%s%d" % (side, first), tag)
             cols = slice(first // LIST_ROWS, (first + count) // LIST_ROWS)
-            nc.vector.tensor_copy(picked[side, first][:], table_scales[:].indirect(which[:, cols]))
+            nc.vector.tensor_copy(picked[side, first][:], table_scales[:].indirect(offsets[side][:, cols]))
+
+        planes = {}
 
         def place_scales(side, first, count, a):
             planes[side, first, a] = held([P, count], U8, "plane_%s%d_%d" % (side, first, a))
@@ -96,93 +104,74 @@ def tile_list_complex_kinship_scores_kernel(
                     picked[side, first][source : source + 64, :].bitcast(I32),
                 )
 
-        tail_words = {}
-
-        def gather_tail_words(c, tag=None):
-            for a in range(PASSES):
-                tail_words[c, a] = held([P, CHUNK], U16, "tail_words%d_%d" % (c, a), tag if a == 0 else None)
-                gather_words("tail", a, c * CHUNK, CHUNK, tail_words[c, a][:])
-
-        head_words = {}
-
-        def gather_head_words(pieces, tag):
-            words = held([P, len(pieces) * CHUNK], U16, "head_words_" + tag, tag)
-            for i, (c, a) in enumerate(pieces):
-                head_words[c, a] = words[:, i * CHUNK : (i + 1) * CHUNK]
-                gather_words("head", a, c * CHUNK, CHUNK, head_words[c, a])
-
-        gather_scales("tail", 0, S)
-        load_wr(0)
-        for a in range(PASSES):
-            place_scales("tail", 0, S, a)
-        load_wr(1)
-        gain_cols = held([P, PACK], F32, "gain_cols")
-        nc.sync.dma_start(gain_cols[:], gain.rearrange("(p t) -> p t", t=PACK))
-        gather_tail_words(0)
+        def gather_words(side, c, a):
+            cols = slice(c * CHUNK // LIST_ROWS, (c + 1) * CHUNK // LIST_ROWS)
+            nc.vector.tensor_copy(words[side, c, a], table_words[a][:].indirect(offsets[side][:, cols]))
 
         codes = {"im": held([P, PASSES * H], I32, "wi_codes"), "re": held([P, PASSES * H], I32, "wr_codes")}
         scales = {"im": held([P, PASSES * H], U8, "wi_plane"), "re": held([P, PASSES * H], U8, "wr_plane")}
-        nc.gpsimd.tensor_copy(
-            scales["im"][:].rearrange("p (a t g m) -> p a g t m", a=PASSES, t=PACK, m=16),
-            wi_scales_raw[:].rearrange("p (a g m t) -> p a g t m", a=PASSES, t=PACK, m=16),
-        )
 
-        for a in range(PASSES):
+        def deal_wi_scales(a):
+            cols = slice(a * H, (a + 1) * H)
+            nc.gpsimd.tensor_copy(
+                scales["im"][:, cols].rearrange("p (t g m) -> p g t m", t=PACK, m=16),
+                wi_scales_raw[:, cols].rearrange("p (g m t) -> p g t m", t=PACK, m=16),
+            )
+
+        def deal_wi_codes(a):
             nc.gpsimd.tensor_copy(
                 codes["im"][:, a * H : (a + 1) * H].rearrange("p (t g m) -> p g t m", t=PACK, m=4),
-                wi_raw[:, a * H : (a + 1) * H].rearrange("p (g m t) -> p g t m", t=PACK, m=4),
+                wi_raw[a][:].rearrange("p (g m t) -> p g t m", t=PACK, m=4),
             )
+
         wr_rounded = [held([P, PACK * H], BF16, "wr_rounded%d" % a) for a in range(PASSES)]
-        for a in range(PASSES):
-            rounded = wr_rounded[a][:].rearrange("p (t m j) -> p t m j", t=PACK, j=PACK)
-            raw = wr_raw[a][:].rearrange("p j (m t) -> p t m j", t=PACK)
-            nc.scalar.copy(
-                rounded[:, 0:3, :, :].rearrange("p t m j -> p m j t"), raw[:, 0:3, :, :].rearrange("p t m j -> p m j t")
-            )
-            nc.gpsimd.tensor_copy(rounded[:, 3, :, :], raw[:, 3, :, :])
 
-        def weight(part, a, t):
-            cols = slice(a * H + t * P, a * H + (t + 1) * P)
-            return codes[part][:, cols].bitcast(FP8X4), scales[part][:, cols]
-
-        tails = {}
-        tail_banks = {}
-
-        def tail_products(part, c):
-            banks = [psum.tile([P, CHUNK], F32, name="bank", tag="bank%d" % (PACK * c + t)) for t in range(PACK)]
-            steps = [(t, a) for t in range(PACK) for a in range(PASSES)]
-            for t, a in steps:
-                if True:
-                    w, w_scale = weight(part, a, t)
-                    nc.tensor.matmul_mx(
-                        out=banks[t][:],
-                        lhsT=w,
-                        lhsT_scale=w_scale,
-                        rhs=tail_words[c, a][:].bitcast(FP4X4),
-                        rhs_scale=planes["tail", 0, a][:, c * CHUNK : (c + 1) * CHUNK],
-                        start=(a == 0),
-                        stop=(a == PASSES - 1),
-                    )
-            tail_banks[part, c] = banks
-
-        def tail_copies(part, c, tag=None):
-            banks = tail_banks[part, c]
-            if c == 0:
-                tails[part] = held([P, 2 * PACK, CHUNK], F32, "tail_%s" % part, tag)
-            tails[part, c] = tails[part][:, PACK * c : PACK * (c + 1), :]
-            for t in range(PACK):
-                nc.scalar.activation(tails[part, c][:, t, :], banks[t][:], COPY, scale=gain_cols[:, t : t + 1])
+        def round_wr(a):
+            rounded = wr_rounded[a][:].rearrange("p (t m j) -> p m t j", t=PACK, j=PACK)
+            raw = wr_raw[a][:].rearrange("p j (m t) -> p m t j", t=PACK)
+            nc.scalar.copy(rounded[:, :SCALAR_SHARE], raw[:, :SCALAR_SHARE])
+            nc.gpsimd.tensor_copy(rounded[:, SCALAR_SHARE:], raw[:, SCALAR_SHARE:])
 
         def quantise_wr(a):
             cols = slice(a * H, (a + 1) * H)
             nc.vector.quantize_mx(out=codes["re"][:, cols].bitcast(FP8X4), scales=scales["re"][:, cols], in_=wr_rounded[a][:])
 
-        products = {}
+        def weight(part, a, t):
+            cols = slice(a * H + t * P, a * H + (t + 1) * P)
+            return codes[part][:, cols].bitcast(FP8X4), scales[part][:, cols]
 
-        def head_products(s):
+        tail_banks = {}
+
+        def tail_pass(part, c, a):
+            if a == 0:
+                tail_banks[part, c] = [bank_tile([P, CHUNK], PACK * c + t) for t in range(PACK)]
+            for t in range(PACK):
+                w, w_scale = weight(part, a, t)
+                nc.tensor.matmul_mx(
+                    out=tail_banks[part, c][t][:],
+                    lhsT=w,
+                    lhsT_scale=w_scale,
+                    rhs=words["tail", c, a].bitcast(FP4X4),
+                    rhs_scale=planes["tail", c * CHUNK, a][:],
+                    start=(a == 0),
+                    stop=(a == PASSES - 1),
+                )
+
+        tails = {}
+
+        def tail_copies(part, c, tag=None):
+            tails[part, c] = held([P, PACK, CHUNK], F32, "tail_%s%d" % (part, c), tag)
+            for t in range(PACK):
+                nc.scalar.activation(tails[part, c][:, t, :], tail_banks[part, c][t][:], COPY, scale=gain_cols[:, t : t + 1])
+
+        products = {}
+        head_banks = {}
+
+        def head_passes(s):
             c, within = divmod(s * STRIP, CHUNK)
             for half, part in enumerate(("im", "re")):
-                bank = psum.tile([P, PACK, STRIP], F32, name="bank", tag="bank%d" % (2 * (s % 2) + half))
+                bank = bank_tile([P, PACK, STRIP], 2 * (s % HEAD_AHEAD) + half)
+                head_banks[part, s] = bank
                 for t in range(PACK):
                     for a in range(PASSES):
                         w, w_scale = weight(part, a, t)
@@ -190,15 +179,19 @@ def tile_list_complex_kinship_scores_kernel(
                             out=bank[:, t, :],
                             lhsT=w,
                             lhsT_scale=w_scale,
-                            rhs=head_words[c, a][:, within : within + STRIP].bitcast(FP4X4),
+                            rhs=words["head", c, a][:, within : within + STRIP].bitcast(FP4X4),
                             rhs_scale=planes["head", 0, a][:, s * STRIP : (s + 1) * STRIP],
                             start=(a == 0),
                             stop=(a == PASSES - 1),
                         )
+
+        def multiply(s):
+            c, within = divmod(s * STRIP, CHUNK)
+            for part in ("im", "re"):
                 products[part, s] = held([P, PACK * STRIP], F32, "product_%s%d" % (part, s))
                 nc.vector.tensor_tensor(
                     products[part, s][:].rearrange("p (g i t) -> p g t i", i=2, t=PACK),
-                    bank[:].rearrange("p t (g i) -> p g t i", i=2),
+                    head_banks[part, s][:].rearrange("p t (g i) -> p g t i", i=2),
                     tails[part, c][:, :, within : within + STRIP].rearrange("p t (g i) -> p g t i", i=2),
                     MULT,
                 )
@@ -212,21 +205,17 @@ def tile_list_complex_kinship_scores_kernel(
                         h_rounded[first] = held([P, PACK * count], BF16, "h_rounded%d" % first)
                     at = PACK * (s * STRIP - first)
                     engine.tensor_tensor(
-                        h_rounded[first][:, at : at + PACK * STRIP],
-                        products["im", s][:],
-                        products["re", s][:],
-                        ADD,
+                        h_rounded[first][:, at : at + PACK * STRIP], products["im", s][:], products["re", s][:], ADD
                     )
 
         def scores(first, count, first_bank):
             h_codes = held([P, count], I32, "h_codes%d" % first)
             h_plane = held([P, count], U8, "h_plane%d" % first)
             nc.vector.quantize_mx(out=h_codes[:].bitcast(FP8X4), scales=h_plane[:], in_=h_rounded[first][:])
-            per_bank = min(CHUNK // count, 2)
             last = first + count == S
-            for n0 in range(0, N // P, per_bank):
-                bank = psum.tile([P, per_bank, count], F32, name="bank", tag="bank%d" % (first_bank + n0 // per_bank))
-                for n in range(n0, n0 + per_bank):
+            for n0 in range(0, N // P, 2):
+                bank = bank_tile([P, 2, count], first_bank + n0 // 2)
+                for n in range(n0, n0 + 2):
                     nc.tensor.matmul_mx(
                         out=bank[:, n - n0, :],
                         lhsT=wrel_codes[:, 2 * P * n : 2 * P * (n + 1)].bitcast(FP4X4),
@@ -236,56 +225,79 @@ def tile_list_complex_kinship_scores_kernel(
                         start=True,
                         stop=True,
                     )
-                if n0 % 2 == 0:
-                    result = held([P, 2, count], F32, "result%d_%d" % (first, n0))
-                for n in range(n0, n0 + per_bank):
+                result = held([P, 2, count], F32, "result%d_%d" % (first, n0))
+                for n in range(n0, n0 + 2):
                     if last and n0 > 0:
-                        nc.vector.tensor_scalar(result[:, n % 2, :], bank[:, n - n0, :], bias_cols[:, n : n + 1], None, ADD)
+                        nc.vector.tensor_scalar(result[:, n - n0, :], bank[:, n - n0, :], bias_cols[:, n : n + 1], None, ADD)
                     else:
-                        nc.scalar.activation(
-                            result[:, n % 2, :], bank[:, n - n0, :], IDENTITY, bias=bias_cols[:, n : n + 1]
-                        )
-                if (n0 + per_bank) % 2 == 0:
-                    rows = slice((n0 // 2) * 2 * P, (n0 // 2 + 1) * 2 * P)
-                    nc.sync.dma_start(out[rows, first : first + count].rearrange("(n p) j -> p n j", p=P), result[:])
+                        nc.scalar.activation(result[:, n - n0, :], bank[:, n - n0, :], IDENTITY, bias=bias_cols[:, n : n + 1])
+                rows = slice(n0 * P, (n0 + 2) * P)
+                nc.sync.dma_start(out[rows, first : first + count].rearrange("(n p) j -> p n j", p=P), result[:])
 
-        tail_products("im", 0)
-        gather_tail_words(1, "wi_raw")
-        tail_products("im", 1)
-        tail_copies("im", 0, "wr_raw1")
-        gather_scales("head", 0, S, "wi_scales_raw")
+        for c in range(2):
+            for a in range(PASSES):
+                words["tail", c, a] = held([P, CHUNK], U16, "tail_words%d_%d" % (c, a))[:]
+        for a in range(PASSES):
+            deal_wi_codes(a)
+            deal_wi_scales(a)
+        gather_scales("tail", 0, CHUNK)
+        place_scales("tail", 0, CHUNK, 0)
+        gain_cols = held([P, PACK], F32, "gain_cols")
+        nc.sync.dma_start(gain_cols[:], gain.rearrange("(p t) -> p t", t=PACK))
+        nc.sync.dma_start(offsets["head"][:], offs)
+        load_wr(0)
+        place_scales("tail", 0, CHUNK, 1)
+        gather_scales("tail", CHUNK, CHUNK)
+        for a in range(PASSES):
+            place_scales("tail", CHUNK, CHUNK, a)
+        load_wr(1)
+        for c in range(2):
+            for a in range(PASSES):
+                gather_words("tail", c, a)
+                tail_pass("im", c, a)
+        round_wr(0)
+        tail_copies("im", 0, "wr_raw0")
+        quantise_wr(0)
+        gather_scales("head", 0, S, "wr_rounded0")
         for a in range(PASSES):
             place_scales("head", 0, S, a)
-        quantise_wr(0)
+        round_wr(1)
         quantise_wr(1)
-        tail_products("re", 0)
-        gather_head_words([(0, 0), (0, 1), (1, 0)], "wr_rounded1")
-        tail_copies("re", 0)
-        tail_copies("im", 1)
-        for s in range(S // STRIP):
-            if s == 4:
-                tail_products("re", 1)
-                tail_copies("re", 1)
-            if s == 3:
-                gather_head_words([(1, 1)], "product_im1")
-                wrel_codes = held([P, 2 * N], U8, "wrel_codes")
-                nc.sync.dma_start(wrel_codes[:].bitcast(I32), wrel_words[0].bitcast(I32))
-                for q in range(4):
-                    nc.sync.dma_start(
-                        wrel_plane[32 * q : 32 * q + 4, :].bitcast(I32), wrel_scales[0, 4 * q : 4 * q + 4, :].bitcast(I32)
-                    )
-                bias_cols = held([P, N // P], F32, "bias_cols")
-                with nc.allow_non_contiguous_dma(reason="one bias value for each output row"):
-                    nc.sync.dma_start(bias_cols[:], bias.rearrange("(n p) -> p n", p=P))
+        tail_copies("im", 1, "wr_raw1")
+        for c in range(2):
+            for a in range(PASSES):
+                tail_pass("re", c, a)
+            tail_copies("re", c)
+        head_words = held([P, 2 * PASSES * CHUNK], U16, "head_words", "wr_rounded1")
+        for c in range(2):
+            for a in range(PASSES):
+                at = (c * PASSES + a) * CHUNK
+                words["head", c, a] = head_words[:, at : at + CHUNK]
+                gather_words("head", c, a)
 
-            if s == 7:
-                scores(512, 256, 4)
-            head_products(s)
-            if s == 4:
-                scores(0, 256, 4)
+        wrel_codes = held([P, 2 * N], U8, "wrel_codes")
+        nc.sync.dma_start(wrel_codes[:].bitcast(I32), wrel_words[0].bitcast(I32))
+        for q in range(4):
+            nc.sync.dma_start(
+                wrel_plane[32 * q : 32 * q + 4, :].bitcast(I32), wrel_scales[0, 4 * q : 4 * q + 4, :].bitcast(I32)
+            )
+        bias_cols = held([P, N // P], F32, "bias_cols")
+        with nc.allow_non_contiguous_dma(reason="one bias value for each output row"):
+            nc.sync.dma_start(bias_cols[:], bias.rearrange("(n p) -> p n", p=P))
+
+        for s in range(HEAD_AHEAD):
+            head_passes(s)
+        for s in range(STRIPS):
+            multiply(s)
+            if s == 3:
+                scores(0, 256, 6)
             if s == 5:
                 scores(256, 256, 6)
+            if s == 6:
+                scores(512, 256, 4)
+            if s + HEAD_AHEAD < STRIPS:
+                head_passes(s + HEAD_AHEAD)
             if s == 7:
-                scores(768, 128, 6)
+                scores(768, 128, 0)
             add_products(s, nc.vector if s == 7 else nc.gpsimd)
-        scores(896, 128, 0)
+        scores(896, 128, 2)

@@ -129,7 +129,9 @@ def tile_list_complex_kinship_scores_kernel(
         def round_wr(a):
             rounded = wr_rounded[a][:].rearrange("p (t m j) -> p m t j", t=PACK, j=PACK)
             raw = wr_raw[a][:].rearrange("p j (m t) -> p m t j", t=PACK)
-            nc.scalar.copy(rounded[:, :SCALAR_SHARE], raw[:, :SCALAR_SHARE])
+            nc.scalar.copy(
+                rounded[:, :SCALAR_SHARE].rearrange("p m t j -> p m j t"), raw[:, :SCALAR_SHARE].rearrange("p m t j -> p m j t")
+            )
             nc.gpsimd.tensor_copy(rounded[:, SCALAR_SHARE:], raw[:, SCALAR_SHARE:])
 
         def quantise_wr(a):

@@ -210,8 +210,8 @@ def tile_list_complex_kinship_scores_kernel(
                         h_rounded[first][:, at : at + PACK * STRIP], products["im", s][:], products["re", s][:], ADD
                     )
 
-        def scores(first, count, first_bank):
-            h_codes = held([P, count], I32, "h_codes%d" % first)
+        def scores(first, count, first_bank, tag=None):
+            h_codes = held([P, count], I32, "h_codes%d" % first, tag)
             h_plane = held([P, count], U8, "h_plane%d" % first)
             nc.vector.quantize_mx(out=h_codes[:].bitcast(FP8X4), scales=h_plane[:], in_=h_rounded[first][:])
             last = first + count == S
@@ -258,11 +258,13 @@ def tile_list_complex_kinship_scores_kernel(
                 gather_words("tail", c, a)
                 tail_pass("im", c, a)
         round_wr(0)
-        tail_copies("im", 0, "wr_raw0")
-        quantise_wr(0)
-        gather_scales("head", 0, S, "wr_rounded0")
+        tail_copies("im", 0)
+        gather_scales("head", 0, S)
         for a in range(PASSES):
             place_scales("head", 0, S, a)
+        quantise_wr(0)
+        words["head", 0, 0] = held([P, CHUNK], U16, "head_words_first", "wr_rounded0")[:]
+        gather_words("head", 0, 0)
         round_wr(1)
         quantise_wr(1)
         tail_copies("im", 1, "wr_raw1")
@@ -270,12 +272,10 @@ def tile_list_complex_kinship_scores_kernel(
             for a in range(PASSES):
                 tail_pass("re", c, a)
             tail_copies("re", c)
-        head_words = held([P, 2 * PASSES * CHUNK], U16, "head_words", "wr_rounded1")
-        for c in range(2):
-            for a in range(PASSES):
-                at = (c * PASSES + a) * CHUNK
-                words["head", c, a] = head_words[:, at : at + CHUNK]
-                gather_words("head", c, a)
+        head_words = held([P, 3 * CHUNK], U16, "head_words", "wr_rounded1")
+        for i, (c, a) in enumerate(((0, 1), (1, 0), (1, 1))):
+            words["head", c, a] = head_words[:, i * CHUNK : (i + 1) * CHUNK]
+            gather_words("head", c, a)
 
         wrel_codes = held([P, 2 * N], U8, "wrel_codes")
         nc.sync.dma_start(wrel_codes[:].bitcast(I32), wrel_words[0].bitcast(I32))
@@ -292,14 +292,14 @@ def tile_list_complex_kinship_scores_kernel(
         for s in range(STRIPS):
             multiply(s)
             if s == 3:
-                scores(0, 256, 6)
+                scores(0, 256, 6, "wr_rounded0")
             if s == 5:
-                scores(256, 256, 6)
+                scores(256, 256, 6, "wr_rounded0")
             if s == 6:
-                scores(512, 256, 4)
+                scores(512, 256, 4, "wr_rounded1")
             if s + HEAD_AHEAD < STRIPS:
                 head_passes(s + HEAD_AHEAD)
             if s == 7:
-                scores(768, 128, 0)
+                scores(768, 128, 0, "wr_rounded1")
             add_products(s, nc.vector if s == 7 else nc.gpsimd)
         scores(896, 128, 2)

@@ -200,11 +200,11 @@ def tile_list_complex_kinship_scores_kernel(
 
         h_rounded = {}
 
-        def add_products(s, engine):
+        def add_products(s, engine, tag=None):
             for first, count in SCORE_GROUPS:
                 if first <= s * STRIP < first + count:
                     if first not in h_rounded:
-                        h_rounded[first] = held([P, PACK * count], BF16, "h_rounded%d" % first)
+                        h_rounded[first] = held([P, PACK * count], BF16, "h_rounded%d" % first, tag)
                     at = PACK * (s * STRIP - first)
                     engine.tensor_tensor(
                         h_rounded[first][:, at : at + PACK * STRIP], products["im", s][:], products["re", s][:], ADD
@@ -214,7 +214,7 @@ def tile_list_complex_kinship_scores_kernel(
             h_codes = held([P, count], I32, "h_codes%d" % first, tag)
             h_plane = held([P, count], U8, "h_plane%d" % first)
             nc.vector.quantize_mx(out=h_codes[:].bitcast(FP8X4), scales=h_plane[:], in_=h_rounded[first][:])
-            last = first + count == S
+            last = count == STRIP
             for n0 in range(0, N // P, 2):
                 bank = bank_tile([P, 2, count], first_bank + n0 // 2)
                 for n in range(n0, n0 + 2):
@@ -295,11 +295,12 @@ def tile_list_complex_kinship_scores_kernel(
                 scores(0, 256, 6, "wr_rounded0")
             if s == 5:
                 scores(256, 256, 6, "wr_rounded0")
-            if s == 6:
-                scores(512, 256, 4, "wr_rounded1")
             if s + HEAD_AHEAD < STRIPS:
                 head_passes(s + HEAD_AHEAD)
-            if s == 7:
-                scores(768, 128, 0, "wr_rounded1")
-            add_products(s, nc.vector if s == 7 else nc.gpsimd)
+            if s < 6:
+                add_products(s, nc.gpsimd)
+        scores(512, 256, 4, "wr_rounded1")
+        add_products(6, nc.vector, "tail_re1")
+        add_products(7, nc.vector)
+        scores(768, 128, 0)
         scores(896, 128, 2)

@@ -27,7 +27,8 @@ LIST_ROWS = 16
 ALIGN = 64
 HEAD_AHEAD = 3
 SCALAR_SHARE = 64
-SCORE_GROUPS = ((0, 256), (256, 256), (512, 256), (768, 128), (896, 128))
+SCORE_GROUPS = ((0, 512), (512, 256), (768, 128), (896, 128))
+PLANE_CUT = 768
 
 
 def tile_list_complex_kinship_scores_kernel(
@@ -95,13 +96,15 @@ def tile_list_complex_kinship_scores_kernel(
 
         planes = {}
 
-        def place_scales(side, first, count, a):
+        def place_scales(side, first, count, a, gathered=None):
+            gathered = first if gathered is None else gathered
+            cols = slice(first - gathered, first - gathered + count)
             planes[side, first, a] = held([P, count], U8, "plane_%s%d_%d" % (side, first, a))
             for h in range(2):
                 source = 16 + 8 * a + 4 * h
                 nc.sync.dma_start(
                     planes[side, first, a][64 * h : 64 * h + 64, :].bitcast(I32),
-                    picked[side, first][source : source + 64, :].bitcast(I32),
+                    picked[side, gathered][source : source + 64, cols].bitcast(I32),
                 )
 
         def gather_words(side, c, a):
@@ -177,19 +180,20 @@ def tile_list_complex_kinship_scores_kernel(
                 for t in range(PACK):
                     for a in range(PASSES):
                         w, w_scale = weight(part, a, t)
+                        start = PLANE_CUT if a == 0 and s * STRIP >= PLANE_CUT else 0
                         nc.tensor.matmul_mx(
                             out=bank[:, t, :],
                             lhsT=w,
                             lhsT_scale=w_scale,
                             rhs=words["head", c, a][:, within : within + STRIP].bitcast(FP4X4),
-                            rhs_scale=planes["head", 0, a][:, s * STRIP : (s + 1) * STRIP],
+                            rhs_scale=planes["head", start, a][:, s * STRIP - start : (s + 1) * STRIP - start],
                             start=(a == 0),
                             stop=(a == PASSES - 1),
                         )
 
-        def multiply(s):
+        def multiply(s, parts=("im", "re")):
             c, within = divmod(s * STRIP, CHUNK)
-            for part in ("im", "re"):
+            for part in parts:
                 products[part, s] = held([P, PACK * STRIP], F32, "product_%s%d" % (part, s))
                 nc.vector.tensor_tensor(
                     products[part, s][:].rearrange("p (g i t) -> p g t i", i=2, t=PACK),
@@ -210,11 +214,17 @@ def tile_list_complex_kinship_scores_kernel(
                         h_rounded[first][:, at : at + PACK * STRIP], products["im", s][:], products["re", s][:], ADD
                     )
 
-        def scores(first, count, first_bank, tag=None):
+        quantised = {}
+
+        def quantise_h(first, count, tag=None):
             h_codes = held([P, count], I32, "h_codes%d" % first, tag)
             h_plane = held([P, count], U8, "h_plane%d" % first)
             nc.vector.quantize_mx(out=h_codes[:].bitcast(FP8X4), scales=h_plane[:], in_=h_rounded[first][:])
-            last = count == STRIP
+            for at in range(0, count, STRIP):
+                quantised[first + at] = h_codes[:, at:], h_plane[:, at:]
+
+        def scores(first, count, first_bank, vector_banks=()):
+            h_codes, h_plane = quantised[first]
             for n0 in range(0, N // P, 2):
                 bank = bank_tile([P, 2, count], first_bank + n0 // 2)
                 for n in range(n0, n0 + 2):
@@ -222,16 +232,17 @@ def tile_list_complex_kinship_scores_kernel(
                         out=bank[:, n - n0, :],
                         lhsT=wrel_codes[:, 2 * P * n : 2 * P * (n + 1)].bitcast(FP4X4),
                         lhsT_scale=wrel_plane[:, P * n : P * (n + 1)],
-                        rhs=h_codes[:].bitcast(FP8X4),
-                        rhs_scale=h_plane[:],
+                        rhs=h_codes[:, :count].bitcast(FP8X4),
+                        rhs_scale=h_plane[:, :count],
                         start=True,
                         stop=True,
                     )
                 result = held([P, 2, count], F32, "result%d_%d" % (first, n0))
-                for n in range(n0, n0 + 2):
-                    if last and n0 > 0:
-                        nc.vector.tensor_scalar(result[:, n - n0, :], bank[:, n - n0, :], bias_cols[:, n : n + 1], None, ADD)
-                    else:
+                if n0 // 2 in vector_banks:
+                    wide_bias = bias_cols[:, n0 : n0 + 2].unsqueeze(2).to_broadcast([P, 2, count])
+                    nc.vector.tensor_tensor(result[:], bank[:], wide_bias, ADD)
+                else:
+                    for n in range(n0, n0 + 2):
                         nc.scalar.activation(result[:, n - n0, :], bank[:, n - n0, :], IDENTITY, bias=bias_cols[:, n : n + 1])
                 rows = slice(n0 * P, (n0 + 2) * P)
                 nc.sync.dma_start(out[rows, first : first + count].rearrange("(n p) j -> p n j", p=P), result[:])
@@ -259,12 +270,13 @@ def tile_list_complex_kinship_scores_kernel(
                 tail_pass("im", c, a)
         round_wr(0)
         tail_copies("im", 0)
-        gather_scales("head", 0, S)
-        for a in range(PASSES):
-            place_scales("head", 0, S, a)
-        quantise_wr(0)
-        words["head", 0, 0] = held([P, CHUNK], U16, "head_words_first", "wr_rounded0")[:]
+        words["head", 0, 0] = held([P, CHUNK], U16, "head_words_first")[:]
         gather_words("head", 0, 0)
+        quantise_wr(0)
+        gather_scales("head", 0, S, "wr_rounded0")
+        place_scales("head", 0, PLANE_CUT, 0)
+        place_scales("head", 0, S, 1)
+        place_scales("head", PLANE_CUT, S - PLANE_CUT, 0, 0)
         round_wr(1)
         quantise_wr(1)
         tail_copies("im", 1, "wr_raw1")
@@ -291,16 +303,21 @@ def tile_list_complex_kinship_scores_kernel(
             head_passes(s)
         for s in range(STRIPS):
             multiply(s)
-            if s == 3:
-                scores(0, 256, 6, "wr_rounded0")
-            if s == 5:
-                scores(256, 256, 6, "wr_rounded0")
             if s + HEAD_AHEAD < STRIPS:
                 head_passes(s + HEAD_AHEAD)
-            if s < 6:
+            if s < 4:
                 add_products(s, nc.gpsimd)
-        scores(512, 256, 4, "wr_rounded1")
+            if s == 5:
+                quantise_h(0, 512, "plane_head0_0")
+                scores(0, 256, 6)
+                scores(256, 256, 4)
+                add_products(4, nc.gpsimd, "h_rounded0")
+                add_products(5, nc.gpsimd)
+        quantise_h(512, 256, "wr_rounded1")
+        scores(512, 256, 6)
         add_products(6, nc.vector, "tail_re1")
         add_products(7, nc.vector)
-        scores(768, 128, 0)
-        scores(896, 128, 2)
+        quantise_h(768, 128)
+        scores(768, 128, 0, (1,))
+        quantise_h(896, 128)
+        scores(896, 128, 2, (1,))

@@ -22,13 +22,23 @@ PACK = 4
 PASSES = K // (P * PACK)
 CHUNK = 512
 STRIP = 128
-STRIPS = S // STRIP
 LIST_ROWS = 16
 ALIGN = 64
-HEAD_AHEAD = 3
-SCALAR_SHARE = 64
-SCORE_GROUPS = ((0, 512), (512, 256), (768, 128), (896, 128))
-PLANE_CUT = 768
+HALF = H // 2
+POOL_STRIPS = 3
+ADD_STRIPS = 2
+SIDES = ["tail", "head"]
+
+AT_ROUNDED = (0, 2048)
+AT_PICKED = 0
+AT_TAIL_WORDS = 4096
+AT_TAIL_IM = 8192
+AT_RAW_SCALAR = (AT_TAIL_IM, None)
+AT_RAW_POOL = 16384
+AT_TAIL_RE = 24576
+AT_WIDE = 32768
+AT_TAIL_LAST = 36864
+AT_PRODUCTS = {"im": 45056, "re": 53248}
 
 
 def tile_list_complex_kinship_scores_kernel(
@@ -38,9 +48,12 @@ def tile_list_complex_kinship_scores_kernel(
     with ExitStack() as ctx:
         lists = ctx.enter_context(tc.tile_pool(name="lists", bufs=1))
         keep = ctx.enter_context(tc.tile_pool(name="keep", bufs=1))
+        shared = ctx.enter_context(tc.tile_pool(name="shared", bufs=1))
         psum = ctx.enter_context(tc.psum_pool(name="psum", bufs=1))
 
-        def held(shape, dtype, name, tag=None):
+        def held(shape, dtype, name, tag=None, at=None):
+            if at is not None:
+                return shared.tile(shape, dtype, name=name, tag=name, align_bytes=ALIGN, offset=at)
             return keep.tile(shape, dtype, name=name, tag=tag or name, align_bytes=ALIGN)
 
         def bank_tile(shape, number):
@@ -58,24 +71,31 @@ def tile_list_complex_kinship_scores_kernel(
             engine.memset(table_scales[rows, :].bitcast(I32), 0)
         wrel_plane = held([P, N], U8, "wrel_plane")
         nc.gpsimd.memset(wrel_plane[:].bitcast(I32), 0)
+        gain_cols = held([P, PACK], F32, "gain_cols")
+        nc.gpsimd.dma_start(gain_cols[:], gain.rearrange("(p t) -> p t", t=PACK))
 
         table_words = [held([P, T], U16, "table_words%d" % a) for a in range(PASSES)]
         wi_raw = [held([P, H], I32, "wi_raw%d" % a) for a in range(PASSES)]
-        wr_raw = [held([P, PACK, H], F32, "wr_raw%d" % a) for a in range(PASSES)]
+        wr_raw = {}
+        for a in range(PASSES):
+            wr_raw[a, 0] = held([P, PACK, HALF], F32, "wr_raw_pool%d" % a, at=AT_RAW_POOL if a else None)
+            wr_raw[a, 1] = held([P, PACK, HALF], F32, "wr_raw_scalar%d" % a, at=AT_RAW_SCALAR[a])
 
         def load_words(a):
             nc.sync.dma_start(table_words[a][:].bitcast(I32), tab_words[a].bitcast(I32))
 
+        def load_wr(a, half):
+            rows = wr[512 * a : 512 * (a + 1), half * HALF : (half + 1) * HALF]
+            nc.sync.dma_start(wr_raw[a, half][:], rows.rearrange("(p j) c -> p j c", j=PACK))
+
         def load_wi(a):
             nc.sync.dma_start(wi_raw[a][:], wi_words[a].rearrange("p c i -> p (c i)").bitcast(I32))
-
-        def load_wr(a):
-            nc.sync.dma_start(wr_raw[a][:], wr[512 * a : 512 * (a + 1), :].rearrange("(p j) c -> p j c", j=PACK))
 
         nc.sync.dma_start(offsets["tail"][:], offs2)
         scale_rows = tab_scales.bitcast(I32).rearrange("a (h q r) c -> q (a h) r c", h=2, q=2)
         for q in range(2):
             nc.sync.dma_start(table_scales[32 * q + 16 : 32 * q + 32, :].bitcast(I32), scale_rows[q])
+        nc.sync.dma_start(offsets["head"][:], offs)
         load_words(0)
         load_wi(0)
         for q in range(4):
@@ -87,55 +107,55 @@ def tile_list_complex_kinship_scores_kernel(
         load_wi(1)
 
         picked = {}
+        planes = {}
         words = {}
 
-        def gather_scales(side, first, count, tag=None):
-            picked[side, first] = held([P, count], U8, "picked_%s%d" % (side, first), tag)
-            cols = slice(first // LIST_ROWS, (first + count) // LIST_ROWS)
-            nc.vector.tensor_copy(picked[side, first][:], table_scales[:].indirect(offsets[side][:, cols]))
+        def gather_scales(side, c):
+            cols = slice(c * CHUNK // LIST_ROWS, (c + 1) * CHUNK // LIST_ROWS)
+            nc.vector.tensor_copy(picked[c][:, SIDES.index(side), :], table_scales[:].indirect(offsets[side][:, cols]))
 
-        planes = {}
-
-        def place_scales(side, first, count, a, gathered=None):
-            gathered = first if gathered is None else gathered
-            cols = slice(first - gathered, first - gathered + count)
-            planes[side, first, a] = held([P, count], U8, "plane_%s%d_%d" % (side, first, a))
+        def place_scales(sides, c, a):
+            plane = held([P, len(sides), CHUNK], U8, "plane_%s%d_%d" % (sides[0], c, a))
+            first = SIDES.index(sides[0])
             for h in range(2):
                 source = 16 + 8 * a + 4 * h
                 nc.sync.dma_start(
-                    planes[side, first, a][64 * h : 64 * h + 64, :].bitcast(I32),
-                    picked[side, gathered][source : source + 64, cols].bitcast(I32),
+                    plane[64 * h : 64 * h + 64].bitcast(I32),
+                    picked[c][source : source + 64, first : first + len(sides), :].bitcast(I32),
                 )
+            for i, side in enumerate(sides):
+                planes[side, c, a] = plane[:, i, :]
 
-        def gather_words(side, c, a):
-            cols = slice(c * CHUNK // LIST_ROWS, (c + 1) * CHUNK // LIST_ROWS)
-            nc.vector.tensor_copy(words[side, c, a], table_words[a][:].indirect(offsets[side][:, cols]))
+        def gather_words(side, c, a, within=0, count=CHUNK):
+            first = c * CHUNK + within
+            cols = slice(first // LIST_ROWS, (first + count) // LIST_ROWS)
+            nc.vector.tensor_copy(
+                words[side, c, a][:, within : within + count], table_words[a][:].indirect(offsets[side][:, cols])
+            )
 
         codes = {"im": held([P, PASSES * H], I32, "wi_codes"), "re": held([P, PASSES * H], I32, "wr_codes")}
         scales = {"im": held([P, PASSES * H], U8, "wi_plane"), "re": held([P, PASSES * H], U8, "wr_plane")}
 
-        def deal_wi_scales(a):
+        def deal_wi(a):
             cols = slice(a * H, (a + 1) * H)
             nc.gpsimd.tensor_copy(
                 scales["im"][:, cols].rearrange("p (t g m) -> p g t m", t=PACK, m=16),
                 wi_scales_raw[:, cols].rearrange("p (g m t) -> p g t m", t=PACK, m=16),
             )
-
-        def deal_wi_codes(a):
             nc.gpsimd.tensor_copy(
-                codes["im"][:, a * H : (a + 1) * H].rearrange("p (t g m) -> p g t m", t=PACK, m=4),
+                codes["im"][:, cols].rearrange("p (t g m) -> p g t m", t=PACK, m=4),
                 wi_raw[a][:].rearrange("p (g m t) -> p g t m", t=PACK, m=4),
             )
 
-        wr_rounded = [held([P, PACK * H], BF16, "wr_rounded%d" % a) for a in range(PASSES)]
+        wr_rounded = {}
 
         def round_wr(a):
-            rounded = wr_rounded[a][:].rearrange("p (t m j) -> p m t j", t=PACK, j=PACK)
-            raw = wr_raw[a][:].rearrange("p j (m t) -> p m t j", t=PACK)
+            wr_rounded[a] = held([P, PACK * H], BF16, "wr_rounded%d" % a, at=AT_ROUNDED[a])
+            rounded = wr_rounded[a][:].rearrange("p (t h m j) -> p h t m j", t=PACK, h=2, j=PACK)
+            nc.gpsimd.tensor_copy(rounded[:, 0], wr_raw[a, 0][:].rearrange("p j (m t) -> p t m j", t=PACK))
             nc.scalar.copy(
-                rounded[:, :SCALAR_SHARE].rearrange("p m t j -> p m j t"), raw[:, :SCALAR_SHARE].rearrange("p m t j -> p m j t")
+                rounded[:, 1].rearrange("p t m j -> p m j t"), wr_raw[a, 1][:].rearrange("p j (m t) -> p m j t", t=PACK)
             )
-            nc.gpsimd.tensor_copy(rounded[:, SCALAR_SHARE:], raw[:, SCALAR_SHARE:])
 
         def quantise_wr(a):
             cols = slice(a * H, (a + 1) * H)
@@ -147,79 +167,84 @@ def tile_list_complex_kinship_scores_kernel(
 
         tail_banks = {}
 
-        def tail_pass(part, c, a):
-            if a == 0:
-                tail_banks[part, c] = [bank_tile([P, CHUNK], PACK * c + t) for t in range(PACK)]
-            for t in range(PACK):
+        def tail_passes(part, c, first_bank, order):
+            tail_banks[part, c] = [bank_tile([P, CHUNK], first_bank + t) for t in range(PACK)]
+            for a, t in order:
                 w, w_scale = weight(part, a, t)
                 nc.tensor.matmul_mx(
                     out=tail_banks[part, c][t][:],
                     lhsT=w,
                     lhsT_scale=w_scale,
                     rhs=words["tail", c, a].bitcast(FP4X4),
-                    rhs_scale=planes["tail", c * CHUNK, a][:],
+                    rhs_scale=planes["tail", c, a],
                     start=(a == 0),
                     stop=(a == PASSES - 1),
                 )
 
+        by_pass = [(a, t) for a in range(PASSES) for t in range(PACK)]
+        by_slice = [(a, t) for t in range(PACK) for a in range(PASSES)]
         tails = {}
 
-        def tail_copies(part, c, tag=None):
-            tails[part, c] = held([P, PACK, CHUNK], F32, "tail_%s%d" % (part, c), tag)
+        def tail_copies(part, c, at=None):
+            tails[part, c] = held([P, PACK, CHUNK], F32, "tail_%s%d" % (part, c), at=at)
             for t in range(PACK):
                 nc.scalar.activation(tails[part, c][:, t, :], tail_banks[part, c][t][:], COPY, scale=gain_cols[:, t : t + 1])
 
-        products = {}
+        products = {part: held([P, PACK * CHUNK], F32, "products_%s" % part, at=AT_PRODUCTS[part]) for part in ("im", "re")}
         head_banks = {}
 
-        def head_passes(s):
+        def head_passes(part, s, number):
             c, within = divmod(s * STRIP, CHUNK)
-            for half, part in enumerate(("im", "re")):
-                bank = bank_tile([P, PACK, STRIP], 2 * (s % HEAD_AHEAD) + half)
-                head_banks[part, s] = bank
-                for t in range(PACK):
-                    for a in range(PASSES):
-                        w, w_scale = weight(part, a, t)
-                        start = PLANE_CUT if a == 0 and s * STRIP >= PLANE_CUT else 0
-                        nc.tensor.matmul_mx(
-                            out=bank[:, t, :],
-                            lhsT=w,
-                            lhsT_scale=w_scale,
-                            rhs=words["head", c, a][:, within : within + STRIP].bitcast(FP4X4),
-                            rhs_scale=planes["head", start, a][:, s * STRIP - start : (s + 1) * STRIP - start],
-                            start=(a == 0),
-                            stop=(a == PASSES - 1),
-                        )
-
-        def multiply(s, parts=("im", "re")):
-            c, within = divmod(s * STRIP, CHUNK)
-            for part in parts:
-                products[part, s] = held([P, PACK * STRIP], F32, "product_%s%d" % (part, s))
-                nc.vector.tensor_tensor(
-                    products[part, s][:].rearrange("p (g i t) -> p g t i", i=2, t=PACK),
-                    head_banks[part, s][:].rearrange("p t (g i) -> p g t i", i=2),
-                    tails[part, c][:, :, within : within + STRIP].rearrange("p t (g i) -> p g t i", i=2),
-                    MULT,
+            bank = bank_tile([P, PACK, STRIP], number)
+            head_banks[part, s] = bank
+            for a, t in by_slice:
+                w, w_scale = weight(part, a, t)
+                nc.tensor.matmul_mx(
+                    out=bank[:, t, :],
+                    lhsT=w,
+                    lhsT_scale=w_scale,
+                    rhs=words["head", c, a][:, within : within + STRIP].bitcast(FP4X4),
+                    rhs_scale=planes["head", c, a][:, within : within + STRIP],
+                    start=(a == 0),
+                    stop=(a == PASSES - 1),
                 )
 
-        h_rounded = {}
+        def strips_of(part, s, count=1):
+            if (part, s) in products:
+                return products[part, s][:]
+            return products[part][:, PACK * STRIP * s : PACK * STRIP * (s + count)]
 
-        def add_products(s, engine, tag=None):
-            for first, count in SCORE_GROUPS:
-                if first <= s * STRIP < first + count:
-                    if first not in h_rounded:
-                        h_rounded[first] = held([P, PACK * count], BF16, "h_rounded%d" % first, tag)
-                    at = PACK * (s * STRIP - first)
-                    engine.tensor_tensor(
-                        h_rounded[first][:, at : at + PACK * STRIP], products["im", s][:], products["re", s][:], ADD
-                    )
+        def multiply(part, s, at=None):
+            c, within = divmod(s * STRIP, CHUNK)
+            if c:
+                products[part, s] = held([P, PACK * STRIP], F32, "product_%s%d" % (part, s), at=at)
+            nc.vector.tensor_tensor(
+                strips_of(part, s).rearrange("p (g i t) -> p g t i", i=2, t=PACK),
+                head_banks[part, s][:].rearrange("p t (g i) -> p g t i", i=2),
+                tails[part, c][:, :, within : within + STRIP].rearrange("p t (g i) -> p g t i", i=2),
+                MULT,
+            )
+
+        def multiply_on_pool(part, s, heads):
+            c, within = divmod(s * STRIP, CHUNK)
+            woven = heads.rearrange("p (j t) -> p j t", t=PACK)
+            nc.scalar.copy(woven, head_banks[part, s][:].rearrange("p t j -> p j t"))
+            nc.gpsimd.tensor_tensor(
+                strips_of(part, s).rearrange("p (j t) -> p j t", t=PACK),
+                woven,
+                tails[part, c][:, :, within : within + STRIP].rearrange("p t j -> p j t"),
+                MULT,
+            )
+
+        def add_products(rounded, s, count, engine):
+            engine.tensor_tensor(rounded, strips_of("im", s, count), strips_of("re", s, count), ADD)
 
         quantised = {}
 
-        def quantise_h(first, count, tag=None):
-            h_codes = held([P, count], I32, "h_codes%d" % first, tag)
+        def quantise_h(first, count, rounded, at=None):
+            h_codes = held([P, count], I32, "h_codes%d" % first, at=at)
             h_plane = held([P, count], U8, "h_plane%d" % first)
-            nc.vector.quantize_mx(out=h_codes[:].bitcast(FP8X4), scales=h_plane[:], in_=h_rounded[first][:])
+            nc.vector.quantize_mx(out=h_codes[:].bitcast(FP8X4), scales=h_plane[:], in_=rounded)
             for at in range(0, count, STRIP):
                 quantised[first + at] = h_codes[:, at:], h_plane[:, at:]
 
@@ -247,47 +272,36 @@ def tile_list_complex_kinship_scores_kernel(
                 rows = slice(n0 * P, (n0 + 2) * P)
                 nc.sync.dma_start(out[rows, first : first + count].rearrange("(n p) j -> p n j", p=P), result[:])
 
-        for c in range(2):
-            for a in range(PASSES):
-                words["tail", c, a] = held([P, CHUNK], U16, "tail_words%d_%d" % (c, a))[:]
         for a in range(PASSES):
-            deal_wi_codes(a)
-            deal_wi_scales(a)
-        gather_scales("tail", 0, CHUNK)
-        place_scales("tail", 0, CHUNK, 0)
-        gain_cols = held([P, PACK], F32, "gain_cols")
-        nc.sync.dma_start(gain_cols[:], gain.rearrange("(p t) -> p t", t=PACK))
-        nc.sync.dma_start(offsets["head"][:], offs)
-        load_wr(0)
-        place_scales("tail", 0, CHUNK, 1)
-        gather_scales("tail", CHUNK, CHUNK)
+            deal_wi(a)
+            for side in ("tail", "head"):
+                words[side, 0, a] = held([P, CHUNK], U16, "%s_words%d" % (side, a))[:]
+        picked[0] = held([P, 2, CHUNK], U8, "picked_first")
+        for side in SIDES:
+            gather_scales(side, 0)
+        place_scales(["tail"], 0, 0)
+        load_wr(0, 0)
+        place_scales(SIDES, 0, 1)
+        load_wr(0, 1)
+        place_scales(["head"], 0, 0)
+        load_wr(1, 0)
+        load_wr(1, 1)
         for a in range(PASSES):
-            place_scales("tail", CHUNK, CHUNK, a)
-        load_wr(1)
-        for c in range(2):
-            for a in range(PASSES):
-                gather_words("tail", c, a)
-                tail_pass("im", c, a)
+            gather_words("tail", 0, a)
+            gather_words("head", 0, a)
+        tail_passes("im", 0, 0, by_pass)
+        for s in range(4):
+            head_passes("im", s, 4 + s)
         round_wr(0)
-        tail_copies("im", 0)
-        words["head", 0, 0] = held([P, CHUNK], U16, "head_words_first")[:]
-        gather_words("head", 0, 0)
         quantise_wr(0)
-        gather_scales("head", 0, S, "wr_rounded0")
-        place_scales("head", 0, PLANE_CUT, 0)
-        place_scales("head", 0, S, 1)
-        place_scales("head", PLANE_CUT, S - PLANE_CUT, 0, 0)
+        tail_copies("im", 0, AT_TAIL_IM)
         round_wr(1)
+        picked[1] = held([P, 2, CHUNK], U8, "picked_next", at=AT_PICKED)
+        for side in SIDES:
+            gather_scales(side, 1)
+        for a in range(PASSES):
+            place_scales(SIDES, 1, a)
         quantise_wr(1)
-        tail_copies("im", 1, "wr_raw1")
-        for c in range(2):
-            for a in range(PASSES):
-                tail_pass("re", c, a)
-            tail_copies("re", c)
-        head_words = held([P, 3 * CHUNK], U16, "head_words", "wr_rounded1")
-        for i, (c, a) in enumerate(((0, 1), (1, 0), (1, 1))):
-            words["head", c, a] = head_words[:, i * CHUNK : (i + 1) * CHUNK]
-            gather_words("head", c, a)
 
         wrel_codes = held([P, 2 * N], U8, "wrel_codes")
         nc.sync.dma_start(wrel_codes[:].bitcast(I32), wrel_words[0].bitcast(I32))
@@ -299,25 +313,57 @@ def tile_list_complex_kinship_scores_kernel(
         with nc.allow_non_contiguous_dma(reason="one bias value for each output row"):
             nc.sync.dma_start(bias_cols[:], bias.rearrange("(n p) -> p n", p=P))
 
-        for s in range(HEAD_AHEAD):
-            head_passes(s)
-        for s in range(STRIPS):
-            multiply(s)
-            if s + HEAD_AHEAD < STRIPS:
-                head_passes(s + HEAD_AHEAD)
-            if s < 4:
-                add_products(s, nc.gpsimd)
-            if s == 5:
-                quantise_h(0, 512, "plane_head0_0")
-                scores(0, 256, 6)
-                scores(256, 256, 4)
-                add_products(4, nc.gpsimd, "h_rounded0")
-                add_products(5, nc.gpsimd)
-        quantise_h(512, 256, "wr_rounded1")
-        scores(512, 256, 6)
-        add_products(6, nc.vector, "tail_re1")
-        add_products(7, nc.vector)
-        quantise_h(768, 128)
-        scores(768, 128, 0, (1,))
-        quantise_h(896, 128)
-        scores(896, 128, 2, (1,))
+        tail_passes("re", 0, 0, by_pass)
+        for s in range(4 - POOL_STRIPS):
+            multiply("im", s)
+        if POOL_STRIPS:
+            heads = held([P, POOL_STRIPS, PACK * STRIP], F32, "heads_im", at=AT_RAW_POOL)
+            for i in range(POOL_STRIPS):
+                multiply_on_pool("im", 4 - POOL_STRIPS + i, heads[:, i, :])
+        words["tail", 1, 0] = held([P, CHUNK], U16, "tail_words_next", at=AT_TAIL_WORDS)[:]
+        gather_words("tail", 1, 0)
+        for s in range(4):
+            head_passes("re", s, 4 + s)
+        tail_copies("re", 0, AT_TAIL_RE)
+        words["tail", 1, 1] = held([P, CHUNK], U16, "tail_words_last", "tail_words1")[:]
+        gather_words("tail", 1, 1)
+        tail_passes("im", 1, 0, by_slice)
+        wide = held([P, PACK * CHUNK], BF16, "h_rounded_wide", at=AT_WIDE)
+        for s in range(4):
+            multiply("re", s)
+            if (s + 1) % ADD_STRIPS == 0:
+                first = s + 1 - ADD_STRIPS
+                add_products(wide[:, PACK * STRIP * first : PACK * STRIP * (s + 1)], first, ADD_STRIPS, nc.gpsimd)
+        tail_copies("im", 1)
+        tail_passes("re", 1, 4, by_slice)
+        tail_copies("re", 1, AT_TAIL_LAST)
+        for a in range(PASSES):
+            words["head", 1, a] = held([P, CHUNK], U16, "head_words_next%d" % a, at=AT_TAIL_RE + 2 * CHUNK * a)[:]
+        for within in (0, CHUNK // 2):
+            for a in range(PASSES):
+                gather_words("head", 1, a, within, CHUNK // 2)
+        for s in range(4, 8):
+            head_passes("im", s, 2 * (s - 4))
+            head_passes("re", s, 2 * (s - 4) + 1)
+        for part in ("im", "re"):
+            multiply(part, 4)
+        multiply("im", 5)
+        quantise_h(0, CHUNK, wide[:])
+        scores(0, 256, 0)
+        middle = held([P, PACK * 256], BF16, "h_rounded_middle", at=AT_WIDE)
+        add_products(middle[:, : PACK * STRIP], 4, 1, nc.gpsimd)
+        multiply("re", 5, AT_WIDE + 2048)
+        scores(256, 256, 2)
+        add_products(middle[:, PACK * STRIP :], 5, 1, nc.gpsimd)
+        for s in (6, 7):
+            for part in ("im", "re"):
+                multiply(part, s, AT_PRODUCTS[part] + 2048 * (s - 4))
+        quantise_h(512, 256, middle[:], AT_TAIL_LAST)
+        scores(512, 256, 4)
+        last = [held([P, PACK * STRIP], BF16, "h_rounded_last%d" % i, at=AT_TAIL_LAST + 1024 * (i + 1)) for i in range(2)]
+        add_products(last[0][:], 6, 1, nc.vector)
+        add_products(last[1][:], 7, 1, nc.vector)
+        quantise_h(768, 128, last[0][:])
+        scores(768, 128, 6, (1,))
+        quantise_h(896, 128, last[1][:])
+        scores(896, 128, 0, (1,))

@@ -25,20 +25,20 @@ STRIP = 128
 LIST_ROWS = 16
 ALIGN = 64
 HALF = H // 2
-POOL_STRIPS = 3
 ADD_STRIPS = 2
 SIDES = ["tail", "head"]
 
 AT_ROUNDED = (0, 2048)
-AT_PICKED = 0
-AT_TAIL_WORDS = 4096
+AT_TAIL_PICKED = 0
 AT_TAIL_IM = 8192
 AT_RAW_SCALAR = (AT_TAIL_IM, None)
 AT_RAW_POOL = 16384
 AT_TAIL_RE = 24576
 AT_WIDE = 32768
 AT_TAIL_LAST = 36864
-AT_PRODUCTS = {"im": 45056, "re": 53248}
+AT_PRODUCTS = 45056
+AT_POOL_PRODUCTS = 4096
+AT_HEAD_PICKED = 2048
 
 
 def tile_list_complex_kinship_scores_kernel(
@@ -112,19 +112,22 @@ def tile_list_complex_kinship_scores_kernel(
 
         def gather_scales(side, c):
             cols = slice(c * CHUNK // LIST_ROWS, (c + 1) * CHUNK // LIST_ROWS)
-            nc.vector.tensor_copy(picked[c][:, SIDES.index(side), :], table_scales[:].indirect(offsets[side][:, cols]))
+            nc.vector.tensor_copy(picked[side, c], table_scales[:].indirect(offsets[side][:, cols]))
 
-        def place_scales(sides, c, a):
+        def place_scales(sides, c, a, rows):
             plane = held([P, len(sides), CHUNK], U8, "plane_%s%d_%d" % (sides[0], c, a))
-            first = SIDES.index(sides[0])
             for h in range(2):
                 source = 16 + 8 * a + 4 * h
-                nc.sync.dma_start(
-                    plane[64 * h : 64 * h + 64].bitcast(I32),
-                    picked[c][source : source + 64, first : first + len(sides), :].bitcast(I32),
-                )
+                nc.sync.dma_start(plane[64 * h : 64 * h + 64].bitcast(I32), rows[source : source + 64].bitcast(I32))
             for i, side in enumerate(sides):
                 planes[side, c, a] = plane[:, i, :]
+
+        def later_scales(side, at):
+            rows = held([P, 1, CHUNK], U8, "picked_%s" % side, at=at)
+            picked[side, 1] = rows[:, 0, :]
+            gather_scales(side, 1)
+            for a in range(PASSES):
+                place_scales([side], 1, a, rows)
 
         def gather_words(side, c, a, within=0, count=CHUNK):
             first = c * CHUNK + within
@@ -168,7 +171,8 @@ def tile_list_complex_kinship_scores_kernel(
         tail_banks = {}
 
         def tail_passes(part, c, first_bank, order):
-            tail_banks[part, c] = [bank_tile([P, CHUNK], first_bank + t) for t in range(PACK)]
+            if (part, c) not in tail_banks:
+                tail_banks[part, c] = [bank_tile([P, CHUNK], first_bank + t) for t in range(PACK)]
             for a, t in order:
                 w, w_scale = weight(part, a, t)
                 nc.tensor.matmul_mx(
@@ -190,34 +194,38 @@ def tile_list_complex_kinship_scores_kernel(
             for t in range(PACK):
                 nc.scalar.activation(tails[part, c][:, t, :], tail_banks[part, c][t][:], COPY, scale=gain_cols[:, t : t + 1])
 
-        products = {part: held([P, PACK * CHUNK], F32, "products_%s" % part, at=AT_PRODUCTS[part]) for part in ("im", "re")}
+        products = {}
         head_banks = {}
 
-        def head_passes(part, s, number):
+        def head_passes(part, s, number, order=by_slice):
             c, within = divmod(s * STRIP, CHUNK)
-            bank = bank_tile([P, PACK, STRIP], number)
-            head_banks[part, s] = bank
-            for a, t in by_slice:
+            if (part, s) not in head_banks:
+                head_banks[part, s] = bank_tile([P, PACK, STRIP], number)
+            one_group = len(order) == PACK
+            for a, t in order:
                 w, w_scale = weight(part, a, t)
                 nc.tensor.matmul_mx(
-                    out=bank[:, t, :],
+                    out=head_banks[part, s][:, t, :],
                     lhsT=w,
                     lhsT_scale=w_scale,
                     rhs=words["head", c, a][:, within : within + STRIP].bitcast(FP4X4),
                     rhs_scale=planes["head", c, a][:, within : within + STRIP],
-                    start=(a == 0),
-                    stop=(a == PASSES - 1),
+                    start=(a == 0 and (t == 0 or not one_group)),
+                    stop=(a == PASSES - 1 and (t == PACK - 1 or not one_group)),
                 )
 
+        def product_tile(part, first, count, at=None):
+            tile = held([P, PACK * STRIP * count], F32, "products_%s%d" % (part, first), at=at)
+            for i in range(count):
+                products[part, first + i] = tile[:, PACK * STRIP * i :]
+
         def strips_of(part, s, count=1):
-            if (part, s) in products:
-                return products[part, s][:]
-            return products[part][:, PACK * STRIP * s : PACK * STRIP * (s + count)]
+            return products[part, s][:, : PACK * STRIP * count]
 
         def multiply(part, s, at=None):
             c, within = divmod(s * STRIP, CHUNK)
             if c:
-                products[part, s] = held([P, PACK * STRIP], F32, "product_%s%d" % (part, s), at=at)
+                product_tile(part, s, 1, at)
             nc.vector.tensor_tensor(
                 strips_of(part, s).rearrange("p (g i t) -> p g t i", i=2, t=PACK),
                 head_banks[part, s][:].rearrange("p t (g i) -> p g t i", i=2),
@@ -276,14 +284,15 @@ def tile_list_complex_kinship_scores_kernel(
             deal_wi(a)
             for side in ("tail", "head"):
                 words[side, 0, a] = held([P, CHUNK], U16, "%s_words%d" % (side, a))[:]
-        picked[0] = held([P, 2, CHUNK], U8, "picked_first")
-        for side in SIDES:
+        both = held([P, 2, CHUNK], U8, "picked_first")
+        for i, side in enumerate(SIDES):
+            picked[side, 0] = both[:, i, :]
             gather_scales(side, 0)
-        place_scales(["tail"], 0, 0)
+        place_scales(["tail"], 0, 0, both[:, :1, :])
         load_wr(0, 0)
-        place_scales(SIDES, 0, 1)
+        place_scales(SIDES, 0, 1, both)
         load_wr(0, 1)
-        place_scales(["head"], 0, 0)
+        place_scales(["head"], 0, 0, both[:, 1:, :])
         load_wr(1, 0)
         load_wr(1, 1)
         for a in range(PASSES):
@@ -292,15 +301,16 @@ def tile_list_complex_kinship_scores_kernel(
         tail_passes("im", 0, 0, by_pass)
         for s in range(4):
             head_passes("im", s, 4 + s)
+        words["tail", 1, 0] = held([P, CHUNK], U16, "tail_words_next", "picked_first")[:]
+        gather_words("tail", 1, 0)
         round_wr(0)
         quantise_wr(0)
         tail_copies("im", 0, AT_TAIL_IM)
         round_wr(1)
-        picked[1] = held([P, 2, CHUNK], U8, "picked_next", at=AT_PICKED)
-        for side in SIDES:
-            gather_scales(side, 1)
-        for a in range(PASSES):
-            place_scales(SIDES, 1, a)
+        later_scales("tail", AT_TAIL_PICKED)
+        product_tile("im", 0, 2)
+        for s in range(2):
+            multiply("im", s)
         quantise_wr(1)
 
         wrel_codes = held([P, 2 * N], U8, "wrel_codes")
@@ -313,21 +323,20 @@ def tile_list_complex_kinship_scores_kernel(
         with nc.allow_non_contiguous_dma(reason="one bias value for each output row"):
             nc.sync.dma_start(bias_cols[:], bias.rearrange("(n p) -> p n", p=P))
 
-        tail_passes("re", 0, 0, by_pass)
-        for s in range(4 - POOL_STRIPS):
-            multiply("im", s)
-        if POOL_STRIPS:
-            heads = held([P, POOL_STRIPS, PACK * STRIP], F32, "heads_im", at=AT_RAW_POOL)
-            for i in range(POOL_STRIPS):
-                multiply_on_pool("im", 4 - POOL_STRIPS + i, heads[:, i, :])
-        words["tail", 1, 0] = held([P, CHUNK], U16, "tail_words_next", at=AT_TAIL_WORDS)[:]
-        gather_words("tail", 1, 0)
-        for s in range(4):
-            head_passes("re", s, 4 + s)
+        heads = held([P, 2, PACK * STRIP], F32, "heads_im", at=AT_RAW_POOL)
+        product_tile("im", 2, 2, AT_POOL_PRODUCTS)
+        for i in range(2):
+            multiply_on_pool("im", 2 + i, heads[:, i, :])
+        later_scales("head", AT_HEAD_PICKED)
+        for a in range(PASSES):
+            tail_passes("re", 0, 0, by_pass[PACK * a : PACK * (a + 1)])
+            for s in range(4):
+                head_passes("re", s, 4 + s, by_pass[PACK * a : PACK * (a + 1)])
         tail_copies("re", 0, AT_TAIL_RE)
         words["tail", 1, 1] = held([P, CHUNK], U16, "tail_words_last", "tail_words1")[:]
         gather_words("tail", 1, 1)
         tail_passes("im", 1, 0, by_slice)
+        product_tile("re", 0, 4, AT_PRODUCTS)
         wide = held([P, PACK * CHUNK], BF16, "h_rounded_wide", at=AT_WIDE)
         for s in range(4):
             multiply("re", s)
@@ -357,7 +366,7 @@ def tile_list_complex_kinship_scores_kernel(
         add_products(middle[:, PACK * STRIP :], 5, 1, nc.gpsimd)
         for s in (6, 7):
             for part in ("im", "re"):
-                multiply(part, s, AT_PRODUCTS[part] + 2048 * (s - 4))
+                multiply(part, s, AT_PRODUCTS + 4096 * (s - 6) + (2048 if part == "re" else 0))
         quantise_h(512, 256, middle[:], AT_TAIL_LAST)
         scores(512, 256, 4)
         last = [held([P, PACK * STRIP], BF16, "h_rounded_last%d" % i, at=AT_TAIL_LAST + 1024 * (i + 1)) for i in range(2)]

@@ -24,15 +24,12 @@ CHUNK = 512
 STRIP = 128
 LIST_ROWS = 16
 ALIGN = 64
-HALF = H // 2
+SHARES = (((0, 64, "pool"), (64, 128, "pool")), ((0, 96, "pool"), (96, 128, "scalar")))
 ADD_STRIPS = 2
 SIDES = ["tail", "head"]
 
 AT_ROUNDED = (0, 2048)
 AT_TAIL_PICKED = 0
-AT_TAIL_IM = 8192
-AT_RAW_SCALAR = (AT_TAIL_IM, None)
-AT_RAW_POOL = 16384
 AT_TAIL_RE = 24576
 AT_WIDE = 32768
 AT_TAIL_LAST = 36864
@@ -78,14 +75,15 @@ def tile_list_complex_kinship_scores_kernel(
         wi_raw = [held([P, H], I32, "wi_raw%d" % a) for a in range(PASSES)]
         wr_raw = {}
         for a in range(PASSES):
-            wr_raw[a, 0] = held([P, PACK, HALF], F32, "wr_raw_pool%d" % a, at=AT_RAW_POOL if a else None)
-            wr_raw[a, 1] = held([P, PACK, HALF], F32, "wr_raw_scalar%d" % a, at=AT_RAW_SCALAR[a])
+            for i, (first, last, engine) in enumerate(SHARES[a]):
+                wr_raw[a, i] = held([P, PACK, PACK * (last - first)], F32, "wr_raw%d_%d" % (a, i))
 
         def load_words(a):
             nc.sync.dma_start(table_words[a][:].bitcast(I32), tab_words[a].bitcast(I32))
 
         def load_wr(a, half):
-            rows = wr[512 * a : 512 * (a + 1), half * HALF : (half + 1) * HALF]
+            first, last, engine = SHARES[a][half]
+            rows = wr[512 * a : 512 * (a + 1), PACK * first : PACK * last]
             nc.sync.dma_start(wr_raw[a, half][:], rows.rearrange("(p j) c -> p j c", j=PACK))
 
         def load_wi(a):
@@ -154,11 +152,14 @@ def tile_list_complex_kinship_scores_kernel(
 
         def round_wr(a):
             wr_rounded[a] = held([P, PACK * H], BF16, "wr_rounded%d" % a, at=AT_ROUNDED[a])
-            rounded = wr_rounded[a][:].rearrange("p (t h m j) -> p h t m j", t=PACK, h=2, j=PACK)
-            nc.gpsimd.tensor_copy(rounded[:, 0], wr_raw[a, 0][:].rearrange("p j (m t) -> p t m j", t=PACK))
-            nc.scalar.copy(
-                rounded[:, 1].rearrange("p t m j -> p m j t"), wr_raw[a, 1][:].rearrange("p j (m t) -> p m j t", t=PACK)
-            )
+            rounded = wr_rounded[a][:].rearrange("p (t m j) -> p m t j", t=PACK, j=PACK)
+            for i, (first, last, engine) in enumerate(SHARES[a]):
+                raw = wr_raw[a, i][:].rearrange("p j (m t) -> p m t j", t=PACK)
+                share = rounded[:, first:last]
+                if engine == "pool":
+                    nc.gpsimd.tensor_copy(share, raw)
+                else:
+                    nc.scalar.copy(share.rearrange("p m t j -> p m j t"), raw.rearrange("p m t j -> p m j t"))
 
         def quantise_wr(a):
             cols = slice(a * H, (a + 1) * H)
@@ -233,13 +234,17 @@ def tile_list_complex_kinship_scores_kernel(
                 MULT,
             )
 
-        def multiply_on_pool(part, s, heads):
+        woven = {}
+
+        def weave_heads(part, s):
+            woven[part, s] = held([P, STRIP, PACK], F32, "heads_%s%d" % (part, s))
+            nc.scalar.copy(woven[part, s][:], head_banks[part, s][:].rearrange("p t j -> p j t"))
+
+        def multiply_on_pool(part, s):
             c, within = divmod(s * STRIP, CHUNK)
-            woven = heads.rearrange("p (j t) -> p j t", t=PACK)
-            nc.scalar.copy(woven, head_banks[part, s][:].rearrange("p t j -> p j t"))
             nc.gpsimd.tensor_tensor(
                 strips_of(part, s).rearrange("p (j t) -> p j t", t=PACK),
-                woven,
+                woven[part, s][:],
                 tails[part, c][:, :, within : within + STRIP].rearrange("p t j -> p j t"),
                 MULT,
             )
@@ -305,7 +310,9 @@ def tile_list_complex_kinship_scores_kernel(
         gather_words("tail", 1, 0)
         round_wr(0)
         quantise_wr(0)
-        tail_copies("im", 0, AT_TAIL_IM)
+        tail_copies("im", 0)
+        for s in (2, 3):
+            weave_heads("im", s)
         round_wr(1)
         later_scales("tail", AT_TAIL_PICKED)
         product_tile("im", 0, 2)
@@ -323,10 +330,9 @@ def tile_list_complex_kinship_scores_kernel(
         with nc.allow_non_contiguous_dma(reason="one bias value for each output row"):
             nc.sync.dma_start(bias_cols[:], bias.rearrange("(n p) -> p n", p=P))
 
-        heads = held([P, 2, PACK * STRIP], F32, "heads_im", at=AT_RAW_POOL)
         product_tile("im", 2, 2, AT_POOL_PRODUCTS)
-        for i in range(2):
-            multiply_on_pool("im", 2 + i, heads[:, i, :])
+        for s in (2, 3):
+            multiply_on_pool("im", s)
         later_scales("head", AT_HEAD_PICKED)
         for a in range(PASSES):
             tail_passes("re", 0, 0, by_pass[PACK * a : PACK * (a + 1)])

@@ -24,12 +24,15 @@ CHUNK = 512
 STRIP = 128
 LIST_ROWS = 16
 ALIGN = 64
-SHARES = (((0, 64, "pool"), (64, 128, "pool")), ((0, 96, "pool"), (96, 128, "scalar")))
+SHARES = (((0, 80, "scalar"), (80, 128, "pool")), ((0, 80, "pool"), (80, 128, "scalar")))
 ADD_STRIPS = 2
 SIDES = ["tail", "head"]
 
 AT_ROUNDED = (0, 2048)
 AT_TAIL_PICKED = 0
+AT_TAIL_IM = 8192
+AT_RAW_SCALAR = (AT_TAIL_IM, 17408)
+AT_WOVEN = (16384, 18432)
 AT_TAIL_RE = 24576
 AT_WIDE = 32768
 AT_TAIL_LAST = 36864
@@ -76,7 +79,8 @@ def tile_list_complex_kinship_scores_kernel(
         wr_raw = {}
         for a in range(PASSES):
             for i, (first, last, engine) in enumerate(SHARES[a]):
-                wr_raw[a, i] = held([P, PACK, PACK * (last - first)], F32, "wr_raw%d_%d" % (a, i))
+                at = AT_RAW_SCALAR[a] if engine == "scalar" else None
+                wr_raw[a, i] = held([P, PACK, PACK * (last - first)], F32, "wr_raw%d_%d" % (a, i), at=at)
 
         def load_words(a):
             nc.sync.dma_start(table_words[a][:].bitcast(I32), tab_words[a].bitcast(I32))
@@ -236,8 +240,8 @@ def tile_list_complex_kinship_scores_kernel(
 
         woven = {}
 
-        def weave_heads(part, s):
-            woven[part, s] = held([P, STRIP, PACK], F32, "heads_%s%d" % (part, s))
+        def weave_heads(part, s, at):
+            woven[part, s] = held([P, STRIP, PACK], F32, "heads_%s%d" % (part, s), at=at)
             nc.scalar.copy(woven[part, s][:], head_banks[part, s][:].rearrange("p t j -> p j t"))
 
         def multiply_on_pool(part, s):
@@ -310,10 +314,10 @@ def tile_list_complex_kinship_scores_kernel(
         gather_words("tail", 1, 0)
         round_wr(0)
         quantise_wr(0)
-        tail_copies("im", 0)
-        for s in (2, 3):
-            weave_heads("im", s)
+        tail_copies("im", 0, AT_TAIL_IM)
         round_wr(1)
+        for s in (2, 3):
+            weave_heads("im", s, AT_WOVEN[s - 2])
         later_scales("tail", AT_TAIL_PICKED)
         product_tile("im", 0, 2)
         for s in range(2):

@@ -24,14 +24,14 @@ CHUNK = 512
 STRIP = 128
 LIST_ROWS = 16
 ALIGN = 64
-SHARES = (((0, 80, "scalar"), (80, 128, "pool")), ((0, 80, "pool"), (80, 128, "scalar")))
+SHARES = (((0, 72, "scalar"), (72, 128, "pool")), ((0, 80, "pool"), (80, 128, "scalar")))
 ADD_STRIPS = 2
 SIDES = ["tail", "head"]
 
 AT_ROUNDED = (0, 2048)
 AT_TAIL_PICKED = 0
 AT_TAIL_IM = 8192
-AT_RAW_SCALAR = (AT_TAIL_IM, 17408)
+AT_RAW = (AT_TAIL_IM, 16384)
 AT_WOVEN = (16384, 18432)
 AT_TAIL_RE = 24576
 AT_WIDE = 32768
@@ -76,19 +76,13 @@ def tile_list_complex_kinship_scores_kernel(
 
         table_words = [held([P, T], U16, "table_words%d" % a) for a in range(PASSES)]
         wi_raw = [held([P, H], I32, "wi_raw%d" % a) for a in range(PASSES)]
-        wr_raw = {}
-        for a in range(PASSES):
-            for i, (first, last, engine) in enumerate(SHARES[a]):
-                at = AT_RAW_SCALAR[a] if engine == "scalar" else None
-                wr_raw[a, i] = held([P, PACK, PACK * (last - first)], F32, "wr_raw%d_%d" % (a, i), at=at)
+        wr_raw = [held([P, PACK, H], F32, "wr_raw%d" % a, at=AT_RAW[a]) for a in range(PASSES)]
 
         def load_words(a):
             nc.sync.dma_start(table_words[a][:].bitcast(I32), tab_words[a].bitcast(I32))
 
-        def load_wr(a, half):
-            first, last, engine = SHARES[a][half]
-            rows = wr[512 * a : 512 * (a + 1), PACK * first : PACK * last]
-            nc.sync.dma_start(wr_raw[a, half][:], rows.rearrange("(p j) c -> p j c", j=PACK))
+        def load_wr(a):
+            nc.sync.dma_start(wr_raw[a][:], wr[512 * a : 512 * (a + 1), :].rearrange("(p j) c -> p j c", j=PACK))
 
         def load_wi(a):
             nc.sync.dma_start(wi_raw[a][:], wi_words[a].rearrange("p c i -> p (c i)").bitcast(I32))
@@ -157,8 +151,8 @@ def tile_list_complex_kinship_scores_kernel(
         def round_wr(a):
             wr_rounded[a] = held([P, PACK * H], BF16, "wr_rounded%d" % a, at=AT_ROUNDED[a])
             rounded = wr_rounded[a][:].rearrange("p (t m j) -> p m t j", t=PACK, j=PACK)
-            for i, (first, last, engine) in enumerate(SHARES[a]):
-                raw = wr_raw[a, i][:].rearrange("p j (m t) -> p m t j", t=PACK)
+            for first, last, engine in SHARES[a]:
+                raw = wr_raw[a][:].rearrange("p j (m t) -> p m t j", t=PACK)[:, first:last]
                 share = rounded[:, first:last]
                 if engine == "pool":
                     nc.gpsimd.tensor_copy(share, raw)
@@ -298,12 +292,10 @@ def tile_list_complex_kinship_scores_kernel(
             picked[side, 0] = both[:, i, :]
             gather_scales(side, 0)
         place_scales(["tail"], 0, 0, both[:, :1, :])
-        load_wr(0, 0)
+        load_wr(0)
         place_scales(SIDES, 0, 1, both)
-        load_wr(0, 1)
         place_scales(["head"], 0, 0, both[:, 1:, :])
-        load_wr(1, 0)
-        load_wr(1, 1)
+        load_wr(1)
         for a in range(PASSES):
             gather_words("tail", 0, a)
             gather_words("head", 0, a)

@@ -25,7 +25,6 @@ STRIP = 128
 LIST_ROWS = 16
 ALIGN = 64
 SHARES = (((0, 72, "scalar"), (72, 128, "pool")), ((0, 80, "pool"), (80, 128, "scalar")))
-ADD_STRIPS = 2
 SIDES = ["tail", "head"]
 
 AT_ROUNDED = (0, 2048)
@@ -38,6 +37,7 @@ AT_WIDE = 32768
 AT_TAIL_LAST = 36864
 AT_PRODUCTS = 45056
 AT_POOL_PRODUCTS = 4096
+AT_LATE = {("im", 6): AT_PRODUCTS + 4096, ("re", 6): AT_PRODUCTS + 6144, ("im", 7): AT_PRODUCTS, ("re", 7): AT_POOL_PRODUCTS}
 AT_HEAD_PICKED = 2048
 
 
@@ -261,9 +261,10 @@ def tile_list_complex_kinship_scores_kernel(
 
         def scores(first, count, first_bank, vector_banks=()):
             h_codes, h_plane = quantised[first]
-            for n0 in range(0, N // P, 2):
-                bank = bank_tile([P, 2, count], first_bank + n0 // 2)
-                for n in range(n0, n0 + 2):
+            tiles = 1 if count == CHUNK else 2
+            for n0 in range(0, N // P, tiles):
+                bank = bank_tile([P, tiles, count], first_bank + n0 // tiles)
+                for n in range(n0, n0 + tiles):
                     nc.tensor.matmul_mx(
                         out=bank[:, n - n0, :],
                         lhsT=wrel_codes[:, 2 * P * n : 2 * P * (n + 1)].bitcast(FP4X4),
@@ -273,14 +274,14 @@ def tile_list_complex_kinship_scores_kernel(
                         start=True,
                         stop=True,
                     )
-                result = held([P, 2, count], F32, "result%d_%d" % (first, n0))
-                if n0 // 2 in vector_banks:
-                    wide_bias = bias_cols[:, n0 : n0 + 2].unsqueeze(2).to_broadcast([P, 2, count])
+                result = held([P, tiles, count], F32, "result%d_%d" % (first, n0))
+                if n0 // tiles in vector_banks:
+                    wide_bias = bias_cols[:, n0 : n0 + tiles].unsqueeze(2).to_broadcast([P, tiles, count])
                     nc.vector.tensor_tensor(result[:], bank[:], wide_bias, ADD)
                 else:
-                    for n in range(n0, n0 + 2):
+                    for n in range(n0, n0 + tiles):
                         nc.scalar.activation(result[:, n - n0, :], bank[:, n - n0, :], IDENTITY, bias=bias_cols[:, n : n + 1])
-                rows = slice(n0 * P, (n0 + 2) * P)
+                rows = slice(n0 * P, (n0 + tiles) * P)
                 nc.sync.dma_start(out[rows, first : first + count].rearrange("(n p) j -> p n j", p=P), result[:])
 
         for a in range(PASSES):
@@ -330,10 +331,14 @@ def tile_list_complex_kinship_scores_kernel(
         for s in (2, 3):
             multiply_on_pool("im", s)
         later_scales("head", AT_HEAD_PICKED)
-        for a in range(PASSES):
-            tail_passes("re", 0, 0, by_pass[PACK * a : PACK * (a + 1)])
-            for s in range(4):
-                head_passes("re", s, 4 + s, by_pass[PACK * a : PACK * (a + 1)])
+        tail_passes("re", 0, 0, by_pass[:PACK])
+        for s in (0, 1):
+            head_passes("re", s, 4 + s, by_pass[:PACK])
+        tail_passes("re", 0, 0, by_pass[PACK:])
+        for s in (2, 3):
+            head_passes("re", s, 4 + s, by_pass[:PACK])
+        for s in range(4):
+            head_passes("re", s, 4 + s, by_pass[PACK:])
         tail_copies("re", 0, AT_TAIL_RE)
         words["tail", 1, 1] = held([P, CHUNK], U16, "tail_words_last", "tail_words1")[:]
         gather_words("tail", 1, 1)
@@ -342,9 +347,9 @@ def tile_list_complex_kinship_scores_kernel(
         wide = held([P, PACK * CHUNK], BF16, "h_rounded_wide", at=AT_WIDE)
         for s in range(4):
             multiply("re", s)
-            if (s + 1) % ADD_STRIPS == 0:
-                first = s + 1 - ADD_STRIPS
-                add_products(wide[:, PACK * STRIP * first : PACK * STRIP * (s + 1)], first, ADD_STRIPS, nc.gpsimd)
+            if s != 2:
+                first = min(s, 2)
+                add_products(wide[:, PACK * STRIP * first : PACK * STRIP * (s + 1)], first, s + 1 - first, nc.gpsimd)
         tail_copies("im", 1)
         tail_passes("re", 1, 4, by_slice)
         tail_copies("re", 1, AT_TAIL_LAST)
@@ -358,17 +363,16 @@ def tile_list_complex_kinship_scores_kernel(
             head_passes("re", s, 2 * (s - 4) + 1)
         for part in ("im", "re"):
             multiply(part, 4)
-        multiply("im", 5)
         quantise_h(0, CHUNK, wide[:])
-        scores(0, 256, 0)
         middle = held([P, PACK * 256], BF16, "h_rounded_middle", at=AT_WIDE)
         add_products(middle[:, : PACK * STRIP], 4, 1, nc.gpsimd)
-        multiply("re", 5, AT_WIDE + 2048)
-        scores(256, 256, 2)
+        multiply("im", 5, AT_WIDE + 2048)
+        multiply("re", 5, AT_PRODUCTS + 2048)
+        scores(0, CHUNK, 0)
         add_products(middle[:, PACK * STRIP :], 5, 1, nc.gpsimd)
         for s in (6, 7):
             for part in ("im", "re"):
-                multiply(part, s, AT_PRODUCTS + 4096 * (s - 6) + (2048 if part == "re" else 0))
+                multiply(part, s, AT_LATE[part, s])
         quantise_h(512, 256, middle[:], AT_TAIL_LAST)
         scores(512, 256, 4)
         last = [held([P, PACK * STRIP], BF16, "h_rounded_last%d" % i, at=AT_TAIL_LAST + 1024 * (i + 1)) for i in range(2)]

@@ -28,9 +28,8 @@ SHARES = (((0, 72, "scalar"), (72, 128, "pool")), ((0, 80, "pool"), (80, 128, "s
 SIDES = ["tail", "head"]
 
 AT_ROUNDED = (0, 2048)
-AT_TAIL_PICKED = 0
-AT_TAIL_IM = 8192
-AT_RAW = (AT_TAIL_IM, 16384)
+AT_TAIL_IM = 61952
+AT_RAW = (AT_TAIL_IM - 512, 16384)
 AT_WOVEN = (16384, 18432)
 AT_TAIL_RE = 24576
 AT_WIDE = 32768
@@ -38,7 +37,7 @@ AT_TAIL_LAST = 36864
 AT_PRODUCTS = 45056
 AT_POOL_PRODUCTS = 4096
 AT_LATE = {("im", 6): AT_PRODUCTS + 4096, ("re", 6): AT_PRODUCTS + 6144, ("im", 7): AT_PRODUCTS, ("re", 7): AT_POOL_PRODUCTS}
-AT_HEAD_PICKED = 2048
+AT_HEAD_PICKED = 20480
 
 
 def tile_list_complex_kinship_scores_kernel(
@@ -259,11 +258,11 @@ def tile_list_complex_kinship_scores_kernel(
             for at in range(0, count, STRIP):
                 quantised[first + at] = h_codes[:, at:], h_plane[:, at:]
 
-        def scores(first, count, first_bank, vector_banks=()):
+        def scores(first, count, banks, vector_banks=()):
             h_codes, h_plane = quantised[first]
             tiles = 1 if count == CHUNK else 2
             for n0 in range(0, N // P, tiles):
-                bank = bank_tile([P, tiles, count], first_bank + n0 // tiles)
+                bank = bank_tile([P, tiles, count], banks[n0 // tiles])
                 for n in range(n0, n0 + tiles):
                     nc.tensor.matmul_mx(
                         out=bank[:, n - n0, :],
@@ -303,7 +302,7 @@ def tile_list_complex_kinship_scores_kernel(
         tail_passes("im", 0, 0, by_pass)
         for s in range(4):
             head_passes("im", s, 4 + s)
-        words["tail", 1, 0] = held([P, CHUNK], U16, "tail_words_next", "picked_first")[:]
+        words["tail", 1, 0] = held([P, CHUNK], U16, "tail_words_next", "wi_raw1")[:]
         gather_words("tail", 1, 0)
         round_wr(0)
         quantise_wr(0)
@@ -311,7 +310,7 @@ def tile_list_complex_kinship_scores_kernel(
         round_wr(1)
         for s in (2, 3):
             weave_heads("im", s, AT_WOVEN[s - 2])
-        later_scales("tail", AT_TAIL_PICKED)
+        later_scales("tail", AT_RAW[0])
         product_tile("im", 0, 2)
         for s in range(2):
             multiply("im", s)
@@ -358,7 +357,7 @@ def tile_list_complex_kinship_scores_kernel(
         for within in (0, CHUNK // 2):
             for a in range(PASSES):
                 gather_words("head", 1, a, within, CHUNK // 2)
-        for s in range(4, 8):
+        for s in range(4, 7):
             head_passes("im", s, 2 * (s - 4))
             head_passes("re", s, 2 * (s - 4) + 1)
         for part in ("im", "re"):
@@ -366,19 +365,22 @@ def tile_list_complex_kinship_scores_kernel(
         quantise_h(0, CHUNK, wide[:])
         middle = held([P, PACK * 256], BF16, "h_rounded_middle", at=AT_WIDE)
         add_products(middle[:, : PACK * STRIP], 4, 1, nc.gpsimd)
-        multiply("im", 5, AT_WIDE + 2048)
+        multiply("im", 5, AT_POOL_PRODUCTS + 2048)
         multiply("re", 5, AT_PRODUCTS + 2048)
-        scores(0, CHUNK, 0)
+        head_passes("im", 7, 2)
+        head_passes("re", 7, 3)
         add_products(middle[:, PACK * STRIP :], 5, 1, nc.gpsimd)
-        for s in (6, 7):
-            for part in ("im", "re"):
-                multiply(part, s, AT_LATE[part, s])
-        quantise_h(512, 256, middle[:], AT_TAIL_LAST)
-        scores(512, 256, 4)
+        for part in ("im", "re"):
+            multiply(part, 6, AT_LATE[part, 6])
+        scores(0, CHUNK, (6, 7, 4, 5))
+        for part in ("im", "re"):
+            multiply(part, 7, AT_LATE[part, 7])
+        quantise_h(512, 256, middle[:], at=AT_TAIL_RE + 2 * CHUNK)
+        scores(512, 256, (0, 1))
         last = [held([P, PACK * STRIP], BF16, "h_rounded_last%d" % i, at=AT_TAIL_LAST + 1024 * (i + 1)) for i in range(2)]
         add_products(last[0][:], 6, 1, nc.vector)
         add_products(last[1][:], 7, 1, nc.vector)
         quantise_h(768, 128, last[0][:])
-        scores(768, 128, 6, (1,))
+        scores(768, 128, (6, 7), (0, 1))
         quantise_h(896, 128, last[1][:])
-        scores(896, 128, 0, (1,))
+        scores(896, 128, (2, 3), (1,))

@@ -24,7 +24,7 @@ CHUNK = 512
 STRIP = 128
 LIST_ROWS = 16
 ALIGN = 64
-SHARES = (((0, 72, "scalar"), (72, 128, "pool")), ((0, 80, "pool"), (80, 128, "scalar")))
+SHARES = (((0, 56, "scalar"), (56, 128, "pool")), ((0, 72, "pool"), (72, 128, "scalar")))
 SIDES = ["tail", "head"]
 
 AT_ROUNDED = (0, 2048)
@@ -306,7 +306,7 @@ def tile_list_complex_kinship_scores_kernel(
         gather_words("tail", 1, 0)
         round_wr(0)
         quantise_wr(0)
-        tail_copies("im", 0, AT_TAIL_IM)
+        tail_copies("im", 0)
         round_wr(1)
         for s in (2, 3):
             weave_heads("im", s, AT_WOVEN[s - 2])

@@ -156,7 +156,7 @@ def tile_list_complex_kinship_scores_kernel(
                 if engine == "pool":
                     nc.gpsimd.tensor_copy(share, raw)
                 else:
-                    nc.scalar.copy(share.rearrange("p m t j -> p m j t"), raw.rearrange("p m t j -> p m j t"))
+                    nc.scalar.copy(share.rearrange("p m t (u v) -> p m u t v", v=2), raw.rearrange("p m t (u v) -> p m u t v", v=2))
 
         def quantise_wr(a):
             cols = slice(a * H, (a + 1) * H)

@@ -8,6 +8,7 @@ FLOPS = 2 * (4 * K * H * S + H * N * S)
 F32 = mybir.dt.float32
 BF16 = mybir.dt.bfloat16
 I32 = mybir.dt.int32
+U32 = mybir.dt.uint32
 U16 = mybir.dt.uint16
 U8 = mybir.dt.uint8
 FP8X4 = mybir.dt.float8_e4m3fn_x4
@@ -24,7 +25,7 @@ CHUNK = 512
 STRIP = 128
 LIST_ROWS = 16
 ALIGN = 64
-SHARES = (((0, 56, "scalar"), (56, 128, "pool")), ((0, 72, "pool"), (72, 128, "scalar")))
+SHARES = (((0, 64, "scalar"), (64, 128, "pool")), ((0, 72, "pool"), (72, 128, "scalar")))
 SIDES = ["tail", "head"]
 
 AT_ROUNDED = (0, 2048)
@@ -140,9 +141,9 @@ def tile_list_complex_kinship_scores_kernel(
                 scales["im"][:, cols].rearrange("p (t g m) -> p g t m", t=PACK, m=16),
                 wi_scales_raw[:, cols].rearrange("p (g m t) -> p g t m", t=PACK, m=16),
             )
-            nc.gpsimd.tensor_copy(
-                codes["im"][:, cols].rearrange("p (t g m) -> p g t m", t=PACK, m=4),
-                wi_raw[a][:].rearrange("p (g m t) -> p g t m", t=PACK, m=4),
+            nc.scalar.copy(
+                codes["im"][:, cols].bitcast(U32).rearrange("p (t g m) -> p g t m", t=PACK, m=4),
+                wi_raw[a][:].bitcast(U32).rearrange("p (g m t) -> p g t m", t=PACK, m=4),
             )
 
         wr_rounded = {}

@@ -303,8 +303,6 @@ def tile_list_complex_kinship_scores_kernel(
         tail_passes("im", 0, 0, by_pass)
         for s in range(4):
             head_passes("im", s, 4 + s)
-        words["tail", 1, 0] = held([P, CHUNK], U16, "tail_words_next", "wi_raw1")[:]
-        gather_words("tail", 1, 0)
         round_wr(0)
         quantise_wr(0)
         tail_copies("im", 0)
@@ -316,6 +314,9 @@ def tile_list_complex_kinship_scores_kernel(
         for s in range(2):
             multiply("im", s)
         quantise_wr(1)
+        for a in range(PASSES):
+            words["tail", 1, a] = held([P, CHUNK], U16, "tail_words_next%d" % a, at=AT_HEAD_PICKED + 1024 * (a + 1))[:]
+            gather_words("tail", 1, a)
 
         wrel_codes = held([P, 2 * N], U8, "wrel_codes")
         nc.sync.dma_start(wrel_codes[:].bitcast(I32), wrel_words[0].bitcast(I32))
@@ -340,8 +341,6 @@ def tile_list_complex_kinship_scores_kernel(
         for s in range(4):
             head_passes("re", s, 4 + s, by_pass[PACK:])
         tail_copies("re", 0, AT_TAIL_RE)
-        words["tail", 1, 1] = held([P, CHUNK], U16, "tail_words_last", "tail_words1")[:]
-        gather_words("tail", 1, 1)
         tail_passes("im", 1, 0, by_slice)
         product_tile("re", 0, 4, AT_PRODUCTS)
         wide = held([P, PACK * CHUNK], BF16, "h_rounded_wide", at=AT_WIDE)

@@ -125,6 +125,23 @@ def tile_list_complex_kinship_scores_kernel(
             for a in range(PASSES):
                 place_scales([side], 1, a, rows)
 
+        def later_head_scales(half, tag=None, at=None):
+            count = CHUNK // 2
+            rows = held([P, count], U8, "picked_head%d" % half, tag=tag, at=at)
+            first = CHUNK + half * count
+            nc.vector.tensor_copy(
+                rows[:], table_scales[:].indirect(offsets["head"][:, first // LIST_ROWS : (first + count) // LIST_ROWS])
+            )
+            for a in range(PASSES):
+                if half == 0:
+                    planes["head", 1, a] = held([P, CHUNK], U8, "plane_head1_%d" % a)[:]
+                for h in range(2):
+                    source = 16 + 8 * a + 4 * h
+                    nc.sync.dma_start(
+                        planes["head", 1, a][64 * h : 64 * h + 64, half * count : (half + 1) * count].bitcast(I32),
+                        rows[source : source + 64].bitcast(I32),
+                    )
+
         def gather_words(side, c, a, within=0, count=CHUNK):
             first = c * CHUNK + within
             cols = slice(first // LIST_ROWS, (first + count) // LIST_ROWS)
@@ -188,10 +205,14 @@ def tile_list_complex_kinship_scores_kernel(
         by_slice = [(a, t) for t in range(PACK) for a in range(PASSES)]
         tails = {}
 
-        def tail_copies(part, c, at=None):
+        def tail_copies(part, c, at=None, width=CHUNK):
             tails[part, c] = held([P, PACK, CHUNK], F32, "tail_%s%d" % (part, c), at=at)
-            for t in range(PACK):
-                nc.scalar.activation(tails[part, c][:, t, :], tail_banks[part, c][t][:], COPY, scale=gain_cols[:, t : t + 1])
+            for first in range(0, CHUNK, width):
+                cols = slice(first, first + width)
+                for t in range(PACK):
+                    nc.scalar.activation(
+                        tails[part, c][:, t, cols], tail_banks[part, c][t][:, cols], COPY, scale=gain_cols[:, t : t + 1]
+                    )
 
         products = {}
         head_banks = {}
@@ -232,18 +253,17 @@ def tile_list_complex_kinship_scores_kernel(
                 MULT,
             )
 
-        woven = {}
+        def weave_heads(part, first, count, at):
+            woven = held([P, count * STRIP, PACK], F32, "heads_%s%d" % (part, first), at=at)
+            for i in range(count):
+                nc.scalar.copy(woven[:, STRIP * i : STRIP * (i + 1), :], head_banks[part, first + i][:].rearrange("p t j -> p j t"))
+            return woven
 
-        def weave_heads(part, s, at):
-            woven[part, s] = held([P, STRIP, PACK], F32, "heads_%s%d" % (part, s), at=at)
-            nc.scalar.copy(woven[part, s][:], head_banks[part, s][:].rearrange("p t j -> p j t"))
-
-        def multiply_on_pool(part, s):
-            c, within = divmod(s * STRIP, CHUNK)
+        def multiply_on_pool(part, first, count, woven):
             nc.gpsimd.tensor_tensor(
-                strips_of(part, s).rearrange("p (j t) -> p j t", t=PACK),
-                woven[part, s][:],
-                tails[part, c][:, :, within : within + STRIP].rearrange("p t j -> p j t"),
+                strips_of(part, first, count).rearrange("p (j t) -> p j t", t=PACK),
+                woven[:],
+                tails[part, 0][:, :, STRIP * first : STRIP * (first + count)].rearrange("p t j -> p j t"),
                 MULT,
             )
 
@@ -281,8 +301,12 @@ def tile_list_complex_kinship_scores_kernel(
                 else:
                     for n in range(n0, n0 + tiles):
                         nc.scalar.activation(result[:, n - n0, :], bank[:, n - n0, :], IDENTITY, bias=bias_cols[:, n : n + 1])
-                rows = slice(n0 * P, (n0 + tiles) * P)
-                nc.sync.dma_start(out[rows, first : first + count].rearrange("(n p) j -> p n j", p=P), result[:])
+                step = 1 if count == CHUNK // 2 else tiles
+                for n in range(n0, n0 + tiles, step):
+                    nc.sync.dma_start(
+                        out[n * P : (n + step) * P, first : first + count].rearrange("(n p) j -> p n j", p=P),
+                        result[:, n - n0 : n - n0 + step, :],
+                    )
 
         for a in range(PASSES):
             deal_wi(a)
@@ -303,12 +327,12 @@ def tile_list_complex_kinship_scores_kernel(
         tail_passes("im", 0, 0, by_pass)
         for s in range(4):
             head_passes("im", s, 4 + s)
+        later_head_scales(0, tag="wi_raw1")
         round_wr(0)
         quantise_wr(0)
         tail_copies("im", 0)
         round_wr(1)
-        for s in (2, 3):
-            weave_heads("im", s, AT_WOVEN[s - 2])
+        woven = weave_heads("im", 2, 2, AT_WOVEN[0])
         later_scales("tail", AT_RAW[0])
         product_tile("im", 0, 2)
         for s in range(2):
@@ -329,9 +353,8 @@ def tile_list_complex_kinship_scores_kernel(
             nc.sync.dma_start(bias_cols[:], bias.rearrange("(n p) -> p n", p=P))
 
         product_tile("im", 2, 2, AT_POOL_PRODUCTS)
-        for s in (2, 3):
-            multiply_on_pool("im", s)
-        later_scales("head", AT_HEAD_PICKED)
+        multiply_on_pool("im", 2, 2, woven)
+        later_head_scales(1, at=AT_HEAD_PICKED)
         tail_passes("re", 0, 0, by_pass[:PACK])
         for s in (0, 1):
             head_passes("re", s, 4 + s, by_pass[:PACK])
@@ -340,7 +363,7 @@ def tile_list_complex_kinship_scores_kernel(
             head_passes("re", s, 4 + s, by_pass[:PACK])
         for s in range(4):
             head_passes("re", s, 4 + s, by_pass[PACK:])
-        tail_copies("re", 0, AT_TAIL_RE)
+        tail_copies("re", 0, AT_TAIL_RE, CHUNK // 2)
         tail_passes("im", 1, 0, by_slice)
         product_tile("re", 0, 4, AT_PRODUCTS)
         wide = held([P, PACK * CHUNK], BF16, "h_rounded_wide", at=AT_WIDE)
@@ -381,6 +404,6 @@ def tile_list_complex_kinship_scores_kernel(
         add_products(last[0][:], 6, 1, nc.vector)
         add_products(last[1][:], 7, 1, nc.vector)
         quantise_h(768, 128, last[0][:])
-        scores(768, 128, (6, 7), (0, 1))
+        scores(768, 128, (6, 7), (0,))
         quantise_h(896, 128, last[1][:])
         scores(896, 128, (2, 3), (1,))

@@ -234,6 +234,35 @@ def tile_list_complex_kinship_scores_kernel(
                     stop=(a == PASSES - 1 and (t == PACK - 1 or not one_group)),
                 )
 
+        def wide_passes(part, s, u, number, order=None):
+            c, within = divmod(s * STRIP, CHUNK)
+            if (part, s, u) not in head_banks:
+                head_banks[part, s, u] = bank_tile([P, 2, 2 * STRIP], number)
+            for a in order or range(PASSES):
+                for v in range(2):
+                    w, w_scale = weight(part, a, 2 * u + v)
+                    nc.tensor.matmul_mx(
+                        out=head_banks[part, s, u][:, v, :],
+                        lhsT=w,
+                        lhsT_scale=w_scale,
+                        rhs=words["head", c, a][:, within : within + 2 * STRIP].bitcast(FP4X4),
+                        rhs_scale=planes["head", c, a][:, within : within + 2 * STRIP],
+                        start=(a == 0 and v == 0),
+                        stop=(a == PASSES - 1 and v == 1),
+                    )
+
+        def in_pairs(columns, u):
+            return columns.rearrange("p (g t i) -> p g t i", i=2, t=PACK)[:, :, 2 * u : 2 * u + 2, :]
+
+        def multiply_wide(part, s, u):
+            c, within = divmod(s * STRIP, CHUNK)
+            nc.vector.tensor_tensor(
+                in_pairs(strips_of(part, s, 2), u),
+                head_banks[part, s, u][:].rearrange("p v (g i) -> p g v i", i=2),
+                tails[part, c][:, 2 * u : 2 * u + 2, within : within + 2 * STRIP].rearrange("p v (g i) -> p g v i", i=2),
+                MULT,
+            )
+
         def product_tile(part, first, count, at=None):
             tile = held([P, PACK * STRIP * count], F32, "products_%s%d" % (part, first), at=at)
             for i in range(count):
@@ -247,28 +276,33 @@ def tile_list_complex_kinship_scores_kernel(
             if c:
                 product_tile(part, s, 1, at)
             nc.vector.tensor_tensor(
-                strips_of(part, s).rearrange("p (g i t) -> p g t i", i=2, t=PACK),
+                strips_of(part, s).rearrange("p (g t i) -> p g t i", i=2, t=PACK),
                 head_banks[part, s][:].rearrange("p t (g i) -> p g t i", i=2),
                 tails[part, c][:, :, within : within + STRIP].rearrange("p t (g i) -> p g t i", i=2),
                 MULT,
             )
 
-        def weave_heads(part, first, count, at):
-            woven = held([P, count * STRIP, PACK], F32, "heads_%s%d" % (part, first), at=at)
-            for i in range(count):
-                nc.scalar.copy(woven[:, STRIP * i : STRIP * (i + 1), :], head_banks[part, first + i][:].rearrange("p t j -> p j t"))
+        def weave_heads(part, s, at):
+            woven = held([P, 2 * STRIP * PACK], F32, "heads_%s%d" % (part, s), at=at)
+            for u in range(2):
+                nc.scalar.copy(in_pairs(woven[:], u), head_banks[part, s, u][:].rearrange("p v (g i) -> p g v i", i=2))
             return woven
 
         def multiply_on_pool(part, first, count, woven):
             nc.gpsimd.tensor_tensor(
-                strips_of(part, first, count).rearrange("p (j t) -> p j t", t=PACK),
-                woven[:],
-                tails[part, 0][:, :, STRIP * first : STRIP * (first + count)].rearrange("p t j -> p j t"),
+                strips_of(part, first, count).rearrange("p (g t i) -> p g t i", i=2, t=PACK),
+                woven[:].rearrange("p (g t i) -> p g t i", i=2, t=PACK),
+                tails[part, 0][:, :, STRIP * first : STRIP * (first + count)].rearrange("p t (g i) -> p g t i", i=2),
                 MULT,
             )
 
         def add_products(rounded, s, count, engine):
-            engine.tensor_tensor(rounded, strips_of("im", s, count), strips_of("re", s, count), ADD)
+            engine.tensor_tensor(
+                rounded.rearrange("p (g i t) -> p g i t", i=2, t=PACK),
+                strips_of("im", s, count).rearrange("p (g t i) -> p g i t", i=2, t=PACK),
+                strips_of("re", s, count).rearrange("p (g t i) -> p g i t", i=2, t=PACK),
+                ADD,
+            )
 
         quantised = {}
 
@@ -325,18 +359,19 @@ def tile_list_complex_kinship_scores_kernel(
             gather_words("tail", 0, a)
             gather_words("head", 0, a)
         tail_passes("im", 0, 0, by_pass)
-        for s in range(4):
-            head_passes("im", s, 4 + s)
+        for s in (0, 2):
+            for u in range(2):
+                wide_passes("im", s, u, 4 + s + u)
         later_head_scales(0, tag="wi_raw1")
         round_wr(0)
         quantise_wr(0)
         tail_copies("im", 0)
         round_wr(1)
-        woven = weave_heads("im", 2, 2, AT_WOVEN[0])
+        woven = weave_heads("im", 2, AT_WOVEN[0])
         later_scales("tail", AT_RAW[0])
         product_tile("im", 0, 2)
-        for s in range(2):
-            multiply("im", s)
+        for u in range(2):
+            multiply_wide("im", 0, u)
         quantise_wr(1)
         for a in range(PASSES):
             words["tail", 1, a] = held([P, CHUNK], U16, "tail_words_next%d" % a, at=AT_HEAD_PICKED + 1024 * (a + 1))[:]
@@ -354,35 +389,37 @@ def tile_list_complex_kinship_scores_kernel(
 
         product_tile("im", 2, 2, AT_POOL_PRODUCTS)
         multiply_on_pool("im", 2, 2, woven)
-        later_head_scales(1, at=AT_HEAD_PICKED)
         tail_passes("re", 0, 0, by_pass[:PACK])
-        for s in (0, 1):
-            head_passes("re", s, 4 + s, by_pass[:PACK])
+        for u in range(2):
+            wide_passes("re", 0, u, 4 + u, [0])
         tail_passes("re", 0, 0, by_pass[PACK:])
-        for s in (2, 3):
-            head_passes("re", s, 4 + s, by_pass[:PACK])
-        for s in range(4):
-            head_passes("re", s, 4 + s, by_pass[PACK:])
+        for u in range(2):
+            wide_passes("re", 0, u, 4 + u, [1])
+        for u in range(2):
+            wide_passes("re", 2, u, 6 + u)
         tail_copies("re", 0, AT_TAIL_RE, CHUNK // 2)
         tail_passes("im", 1, 0, by_slice)
         product_tile("re", 0, 4, AT_PRODUCTS)
         wide = held([P, PACK * CHUNK], BF16, "h_rounded_wide", at=AT_WIDE)
-        for s in range(4):
-            multiply("re", s)
-            if s != 2:
-                first = min(s, 2)
-                add_products(wide[:, PACK * STRIP * first : PACK * STRIP * (s + 1)], first, s + 1 - first, nc.gpsimd)
+        for s in (0, 2):
+            for u in range(2):
+                multiply_wide("re", s, u)
+            add_products(wide[:, PACK * STRIP * s : PACK * STRIP * (s + 2)], s, 2, nc.gpsimd)
         tail_copies("im", 1)
         tail_passes("re", 1, 4, by_slice)
         tail_copies("re", 1, AT_TAIL_LAST)
         for a in range(PASSES):
             words["head", 1, a] = held([P, CHUNK], U16, "head_words_next%d" % a, at=AT_TAIL_RE + 2 * CHUNK * a)[:]
-        for within in (0, CHUNK // 2):
-            for a in range(PASSES):
-                gather_words("head", 1, a, within, CHUNK // 2)
-        for s in range(4, 7):
+        for a in range(PASSES):
+            gather_words("head", 1, a, 0, CHUNK // 2)
+        later_head_scales(1, at=AT_TAIL_RE + 4 * CHUNK)
+        for a in range(PASSES):
+            gather_words("head", 1, a, CHUNK // 2, CHUNK // 2)
+        for s in range(4, 6):
             head_passes("im", s, 2 * (s - 4))
             head_passes("re", s, 2 * (s - 4) + 1)
+        for u in range(2):
+            wide_passes("im", 6, u, 4 + u)
         for part in ("im", "re"):
             multiply(part, 4)
         quantise_h(0, CHUNK, wide[:])
@@ -390,14 +427,16 @@ def tile_list_complex_kinship_scores_kernel(
         add_products(middle[:, : PACK * STRIP], 4, 1, nc.gpsimd)
         multiply("im", 5, AT_POOL_PRODUCTS + 2048)
         multiply("re", 5, AT_PRODUCTS + 2048)
-        head_passes("im", 7, 2)
-        head_passes("re", 7, 3)
+        for u in range(2):
+            wide_passes("re", 6, u, 2 + u)
         add_products(middle[:, PACK * STRIP :], 5, 1, nc.gpsimd)
-        for part in ("im", "re"):
-            multiply(part, 6, AT_LATE[part, 6])
+        product_tile("im", 6, 2, AT_PRODUCTS + 4096)
+        for u in range(2):
+            multiply_wide("im", 6, u)
         scores(0, CHUNK, (6, 7, 4, 5))
-        for part in ("im", "re"):
-            multiply(part, 7, AT_LATE[part, 7])
+        product_tile("re", 6, 2, AT_TAIL_RE + 4096)
+        for u in range(2):
+            multiply_wide("re", 6, u)
         quantise_h(512, 256, middle[:], at=AT_TAIL_RE + 2 * CHUNK)
         scores(512, 256, (0, 1))
         last = [held([P, PACK * STRIP], BF16, "h_rounded_last%d" % i, at=AT_TAIL_LAST + 1024 * (i + 1)) for i in range(2)]

@@ -25,7 +25,7 @@ CHUNK = 512
 STRIP = 128
 LIST_ROWS = 16
 ALIGN = 64
-SHARES = (((0, 64, "scalar"), (64, 128, "pool")), ((0, 72, "pool"), (72, 128, "scalar")))
+SHARES = (((0, 72, "scalar"), (72, 128, "pool")), ((0, 76, "pool"), (76, 128, "scalar")))
 SIDES = ["tail", "head"]
 
 AT_ROUNDED = (0, 2048)
@@ -87,10 +87,10 @@ def tile_list_complex_kinship_scores_kernel(
         def load_wi(a):
             nc.sync.dma_start(wi_raw[a][:], wi_words[a].rearrange("p c i -> p (c i)").bitcast(I32))
 
-        nc.sync.dma_start(offsets["tail"][:], offs2)
         scale_rows = tab_scales.bitcast(I32).rearrange("a (h q r) c -> q (a h) r c", h=2, q=2)
         for q in range(2):
             nc.sync.dma_start(table_scales[32 * q + 16 : 32 * q + 32, :].bitcast(I32), scale_rows[q])
+        nc.sync.dma_start(offsets["tail"][:], offs2)
         nc.sync.dma_start(offsets["head"][:], offs)
         load_words(0)
         load_wi(0)

@@ -25,7 +25,7 @@ CHUNK = 512
 STRIP = 128
 LIST_ROWS = 16
 ALIGN = 64
-SHARES = (((0, 72, "scalar"), (72, 128, "pool")), ((0, 76, "pool"), (76, 128, "scalar")))
+SHARES = (((0, 56, "scalar"), (56, 128, "pool")), ((0, 76, "pool"), (76, 128, "scalar")))
 SIDES = ["tail", "head"]
 
 AT_ROUNDED = (0, 2048)
@@ -36,7 +36,7 @@ AT_TAIL_RE = 24576
 AT_WIDE = 32768
 AT_TAIL_LAST = 36864
 AT_PRODUCTS = 45056
-AT_POOL_PRODUCTS = 4096
+AT_POOL_PRODUCTS = 6144
 AT_LATE = {("im", 6): AT_PRODUCTS + 4096, ("re", 6): AT_PRODUCTS + 6144, ("im", 7): AT_PRODUCTS, ("re", 7): AT_POOL_PRODUCTS}
 AT_HEAD_PICKED = 20480
 
@@ -118,8 +118,8 @@ def tile_list_complex_kinship_scores_kernel(
             for i, side in enumerate(sides):
                 planes[side, c, a] = plane[:, i, :]
 
-        def later_scales(side, at):
-            rows = held([P, 1, CHUNK], U8, "picked_%s" % side, at=at)
+        def later_scales(side, tag):
+            rows = held([P, 1, CHUNK], U8, "picked_%s" % side, tag=tag)
             picked[side, 1] = rows[:, 0, :]
             gather_scales(side, 1)
             for a in range(PASSES):
@@ -282,17 +282,16 @@ def tile_list_complex_kinship_scores_kernel(
                 MULT,
             )
 
-        def weave_heads(part, s, at):
-            woven = held([P, 2 * STRIP * PACK], F32, "heads_%s%d" % (part, s), at=at)
-            for u in range(2):
-                nc.scalar.copy(in_pairs(woven[:], u), head_banks[part, s, u][:].rearrange("p v (g i) -> p g v i", i=2))
+        def weave_heads(u, at):
+            woven = held([P, STRIP, 2, 2], F32, "heads_im%d" % u, at=at)
+            nc.scalar.copy(woven[:], head_banks["im", 2, u][:].rearrange("p v (g i) -> p g v i", i=2))
             return woven
 
-        def multiply_on_pool(part, first, count, woven):
+        def multiply_on_pool(u, woven):
             nc.gpsimd.tensor_tensor(
-                strips_of(part, first, count).rearrange("p (g t i) -> p g t i", i=2, t=PACK),
-                woven[:].rearrange("p (g t i) -> p g t i", i=2, t=PACK),
-                tails[part, 0][:, :, STRIP * first : STRIP * (first + count)].rearrange("p t (g i) -> p g t i", i=2),
+                in_pairs(strips_of("im", 2, 2), u),
+                woven[:],
+                tails["im", 0][:, 2 * u : 2 * u + 2, 2 * STRIP :].rearrange("p v (g i) -> p g v i", i=2),
                 MULT,
             )
 
@@ -362,20 +361,31 @@ def tile_list_complex_kinship_scores_kernel(
         for s in (0, 2):
             for u in range(2):
                 wide_passes("im", s, u, 4 + s + u)
-        later_head_scales(0, tag="wi_raw1")
+        later_scales("tail", "wi_raw1")
         round_wr(0)
         quantise_wr(0)
         tail_copies("im", 0)
-        round_wr(1)
-        woven = weave_heads("im", 2, AT_WOVEN[0])
-        later_scales("tail", AT_RAW[0])
+        woven = [weave_heads(0, AT_RAW[0] + 1024)]
+        raw = wr_raw[1][:].rearrange("p j (m t) -> p m t j", t=PACK)
+        halves = [held([P, 2, P, PACK], BF16, "wr_rounded1_%d" % u, at=AT_ROUNDED[1] + 1024 + 2048 * u) for u in range(2)]
+        nc.gpsimd.tensor_copy(halves[0][:].rearrange("p t m j -> p m t j"), raw[:, :, :2, :])
+        nc.scalar.copy(
+            halves[1][:].rearrange("p t m (u v) -> p m u t v", v=2), raw[:, :, 2:, :].rearrange("p m t (u v) -> p m u t v", v=2)
+        )
+        woven.append(weave_heads(1, AT_WOVEN[0]))
+        words["tail", 1, 0] = held([P, CHUNK], U16, "tail_words_next0", at=AT_RAW[0])[:]
+        gather_words("tail", 1, 0)
         product_tile("im", 0, 2)
         for u in range(2):
             multiply_wide("im", 0, u)
-        quantise_wr(1)
-        for a in range(PASSES):
-            words["tail", 1, a] = held([P, CHUNK], U16, "tail_words_next%d" % a, at=AT_HEAD_PICKED + 1024 * (a + 1))[:]
-            gather_words("tail", 1, a)
+        for u in range(2):
+            cols = slice(H + u * H // 2, H + (u + 1) * H // 2)
+            nc.vector.quantize_mx(
+                out=codes["re"][:, cols].bitcast(FP8X4), scales=scales["re"][:, cols], in_=halves[u][:].rearrange("p t m j -> p (t m j)")
+            )
+        words["tail", 1, 1] = held([P, CHUNK], U16, "tail_words_next1", at=AT_HEAD_PICKED + 1024)[:]
+        gather_words("tail", 1, 1)
+        later_head_scales(0, at=AT_HEAD_PICKED)
 
         wrel_codes = held([P, 2 * N], U8, "wrel_codes")
         nc.sync.dma_start(wrel_codes[:].bitcast(I32), wrel_words[0].bitcast(I32))
@@ -388,15 +398,15 @@ def tile_list_complex_kinship_scores_kernel(
             nc.sync.dma_start(bias_cols[:], bias.rearrange("(n p) -> p n", p=P))
 
         product_tile("im", 2, 2, AT_POOL_PRODUCTS)
-        multiply_on_pool("im", 2, 2, woven)
+        for u in range(2):
+            multiply_on_pool(u, woven[u])
         tail_passes("re", 0, 0, by_pass[:PACK])
-        for u in range(2):
-            wide_passes("re", 0, u, 4 + u, [0])
+        for s, u in ((2, 0), (0, 0), (0, 1)):
+            wide_passes("re", s, u, 4 + s + u, [0])
         tail_passes("re", 0, 0, by_pass[PACK:])
-        for u in range(2):
-            wide_passes("re", 0, u, 4 + u, [1])
-        for u in range(2):
-            wide_passes("re", 2, u, 6 + u)
+        for s, u in ((0, 0), (0, 1), (2, 0)):
+            wide_passes("re", s, u, 4 + s + u, [1])
+        wide_passes("re", 2, 1, 7)
         tail_copies("re", 0, AT_TAIL_RE, CHUNK // 2)
         tail_passes("im", 1, 0, by_slice)
         product_tile("re", 0, 4, AT_PRODUCTS)

@@ -282,16 +282,17 @@ def tile_list_complex_kinship_scores_kernel(
                 MULT,
             )
 
-        def weave_heads(u, at):
-            woven = held([P, STRIP, 2, 2], F32, "heads_im%d" % u, at=at)
-            nc.scalar.copy(woven[:], head_banks["im", 2, u][:].rearrange("p v (g i) -> p g v i", i=2))
+        def weave_heads(part, s, at):
+            woven = held([P, 2 * STRIP * PACK], F32, "heads_%s%d" % (part, s), at=at)
+            for u in range(2):
+                nc.scalar.copy(in_pairs(woven[:], u), head_banks[part, s, u][:].rearrange("p v (g i) -> p g v i", i=2))
             return woven
 
-        def multiply_on_pool(u, woven):
+        def multiply_on_pool(part, first, count, woven):
             nc.gpsimd.tensor_tensor(
-                in_pairs(strips_of("im", 2, 2), u),
-                woven[:],
-                tails["im", 0][:, 2 * u : 2 * u + 2, 2 * STRIP :].rearrange("p v (g i) -> p g v i", i=2),
+                strips_of(part, first, count).rearrange("p (g t i) -> p g t i", i=2, t=PACK),
+                woven[:].rearrange("p (g t i) -> p g t i", i=2, t=PACK),
+                tails[part, 0][:, :, STRIP * first : STRIP * (first + count)].rearrange("p t (g i) -> p g t i", i=2),
                 MULT,
             )
 
@@ -365,27 +366,27 @@ def tile_list_complex_kinship_scores_kernel(
         round_wr(0)
         quantise_wr(0)
         tail_copies("im", 0)
-        woven = [weave_heads(0, AT_RAW[0] + 1024)]
+        woven = weave_heads("im", 2, AT_RAW[0] + 1024)
         raw = wr_raw[1][:].rearrange("p j (m t) -> p m t j", t=PACK)
         halves = [held([P, 2, P, PACK], BF16, "wr_rounded1_%d" % u, at=AT_ROUNDED[1] + 1024 + 2048 * u) for u in range(2)]
         nc.gpsimd.tensor_copy(halves[0][:].rearrange("p t m j -> p m t j"), raw[:, :, :2, :])
         nc.scalar.copy(
             halves[1][:].rearrange("p t m (u v) -> p m u t v", v=2), raw[:, :, 2:, :].rearrange("p m t (u v) -> p m u t v", v=2)
         )
-        woven.append(weave_heads(1, AT_WOVEN[0]))
         words["tail", 1, 0] = held([P, CHUNK], U16, "tail_words_next0", at=AT_RAW[0])[:]
         gather_words("tail", 1, 0)
         product_tile("im", 0, 2)
         for u in range(2):
             multiply_wide("im", 0, u)
         for u in range(2):
+            if u:
+                later_head_scales(0, at=AT_ROUNDED[1] + 2048)
             cols = slice(H + u * H // 2, H + (u + 1) * H // 2)
             nc.vector.quantize_mx(
                 out=codes["re"][:, cols].bitcast(FP8X4), scales=scales["re"][:, cols], in_=halves[u][:].rearrange("p t m j -> p (t m j)")
             )
         words["tail", 1, 1] = held([P, CHUNK], U16, "tail_words_next1", at=AT_HEAD_PICKED + 1024)[:]
         gather_words("tail", 1, 1)
-        later_head_scales(0, at=AT_HEAD_PICKED)
 
         wrel_codes = held([P, 2 * N], U8, "wrel_codes")
         nc.sync.dma_start(wrel_codes[:].bitcast(I32), wrel_words[0].bitcast(I32))
@@ -398,15 +399,14 @@ def tile_list_complex_kinship_scores_kernel(
             nc.sync.dma_start(bias_cols[:], bias.rearrange("(n p) -> p n", p=P))
 
         product_tile("im", 2, 2, AT_POOL_PRODUCTS)
-        for u in range(2):
-            multiply_on_pool(u, woven[u])
+        multiply_on_pool("im", 2, 2, woven)
         tail_passes("re", 0, 0, by_pass[:PACK])
-        for s, u in ((2, 0), (0, 0), (0, 1)):
+        for s, u in ((2, 0), (0, 0), (2, 1), (0, 1)):
             wide_passes("re", s, u, 4 + s + u, [0])
-        tail_passes("re", 0, 0, by_pass[PACK:])
-        for s, u in ((0, 0), (0, 1), (2, 0)):
-            wide_passes("re", s, u, 4 + s + u, [1])
-        wide_passes("re", 2, 1, 7)
+        for u in range(2):
+            tail_passes("re", 0, 0, [(1, 2 * u), (1, 2 * u + 1)])
+            for s in (0, 2):
+                wide_passes("re", s, u, 4 + s + u, [1])
         tail_copies("re", 0, AT_TAIL_RE, CHUNK // 2)
         tail_passes("im", 1, 0, by_slice)
         product_tile("re", 0, 4, AT_PRODUCTS)

@@ -24,7 +24,7 @@ PASSES = K // (P * PACK)
 CHUNK = 512
 STRIP = 128
 LIST_ROWS = 16
-ALIGN = 64
+ALIGN = 256
 SHARES = (((0, 56, "scalar"), (56, 128, "pool")), ((0, 76, "pool"), (76, 128, "scalar")))
 SIDES = ["tail", "head"]
 

@@ -296,6 +296,14 @@ def tile_list_complex_kinship_scores_kernel(
                 MULT,
             )
 
+        def add_on_pool(rounded, s, count):
+            nc.gpsimd.tensor_tensor(
+                rounded.rearrange("p (g i t) -> p g t i", i=2, t=PACK),
+                strips_of("im", s, count).rearrange("p (g t i) -> p g t i", i=2, t=PACK),
+                strips_of("re", s, count).rearrange("p (g t i) -> p g t i", i=2, t=PACK),
+                ADD,
+            )
+
         def add_products(rounded, s, count, engine):
             engine.tensor_tensor(
                 rounded.rearrange("p (g i t) -> p g i t", i=2, t=PACK),
@@ -414,7 +422,7 @@ def tile_list_complex_kinship_scores_kernel(
         for s in (0, 2):
             for u in range(2):
                 multiply_wide("re", s, u)
-            add_products(wide[:, PACK * STRIP * s : PACK * STRIP * (s + 2)], s, 2, nc.gpsimd)
+            add_on_pool(wide[:, PACK * STRIP * s : PACK * STRIP * (s + 2)], s, 2)
         tail_copies("im", 1)
         tail_passes("re", 1, 4, by_slice)
         tail_copies("re", 1, AT_TAIL_LAST)
@@ -434,12 +442,12 @@ def tile_list_complex_kinship_scores_kernel(
             multiply(part, 4)
         quantise_h(0, CHUNK, wide[:])
         middle = held([P, PACK * 256], BF16, "h_rounded_middle", at=AT_WIDE)
-        add_products(middle[:, : PACK * STRIP], 4, 1, nc.gpsimd)
+        add_on_pool(middle[:, : PACK * STRIP], 4, 1)
         multiply("im", 5, AT_POOL_PRODUCTS + 2048)
         multiply("re", 5, AT_PRODUCTS + 2048)
         for u in range(2):
             wide_passes("re", 6, u, 2 + u)
-        add_products(middle[:, PACK * STRIP :], 5, 1, nc.gpsimd)
+        add_on_pool(middle[:, PACK * STRIP :], 5, 1)
         product_tile("im", 6, 2, AT_PRODUCTS + 4096)
         for u in range(2):
             multiply_wide("im", 6, u)

@@ -65,10 +65,10 @@ def tile_list_complex_kinship_scores_kernel(
         }
 
         wi_scales_raw = held([P, PASSES * H], U8, "wi_scales_raw")
-        nc.gpsimd.memset(wi_scales_raw[:].bitcast(I32), 0)
         table_scales = held([P, T], U8, "table_scales")
         for rows, engine in ((slice(0, 16), nc.gpsimd), (slice(32, 48), nc.gpsimd), (slice(64, P), nc.vector)):
             engine.memset(table_scales[rows, :].bitcast(I32), 0)
+        nc.gpsimd.memset(wi_scales_raw[:].bitcast(I32), 0)
         wrel_plane = held([P, N], U8, "wrel_plane")
         nc.gpsimd.memset(wrel_plane[:].bitcast(I32), 0)
         gain_cols = held([P, PACK], F32, "gain_cols")

from contextlib import ExitStack

import concourse.mybir as mybir

K, H, N, T, S = 1024, 512, 512, 2048, 1024
FLOPS = 2 * (4 * K * H * S + H * N * S)

F32 = mybir.dt.float32
BF16 = mybir.dt.bfloat16
I32 = mybir.dt.int32
U32 = mybir.dt.uint32
U16 = mybir.dt.uint16
U8 = mybir.dt.uint8
FP8X4 = mybir.dt.float8_e4m3fn_x4
FP4X4 = mybir.dt.float4_e2m1fn_x4
MULT = mybir.AluOpType.mult
ADD = mybir.AluOpType.add
COPY = mybir.ActivationFunctionType.Copy
IDENTITY = mybir.ActivationFunctionType.Identity

P = 128
PACK = 4
PASSES = K // (P * PACK)
CHUNK = 512
STRIP = 128
LIST_ROWS = 16
ALIGN = 256
SHARES = (((0, 56, "scalar"), (56, 128, "pool")), ((0, 76, "pool"), (76, 128, "scalar")))
SIDES = ["tail", "head"]

AT_ROUNDED = (0, 2048)
AT_TAIL_IM = 61952
AT_RAW = (AT_TAIL_IM - 512, 16384)
AT_WOVEN = (16384, 18432)
AT_TAIL_RE = 24576
AT_WIDE = 32768
AT_TAIL_LAST = 36864
AT_PRODUCTS = 45056
AT_POOL_PRODUCTS = 6144
AT_LATE = {("im", 6): AT_PRODUCTS + 4096, ("re", 6): AT_PRODUCTS + 6144, ("im", 7): AT_PRODUCTS, ("re", 7): AT_POOL_PRODUCTS}
AT_HEAD_PICKED = 20480


def tile_list_complex_kinship_scores_kernel(
    tc, tab_words, tab_scales, offs, offs2, wr, wi_words, wi_scales, gain, wrel_words, wrel_scales, bias, out
):
    nc = tc.nc
    with ExitStack() as ctx:
        lists = ctx.enter_context(tc.tile_pool(name="lists", bufs=1))
        keep = ctx.enter_context(tc.tile_pool(name="keep", bufs=1))
        shared = ctx.enter_context(tc.tile_pool(name="shared", bufs=1))
        psum = ctx.enter_context(tc.psum_pool(name="psum", bufs=1))

        def held(shape, dtype, name, tag=None, at=None):
            if at is not None:
                return shared.tile(shape, dtype, name=name, tag=name, align_bytes=ALIGN, offset=at)
            return keep.tile(shape, dtype, name=name, tag=tag or name, align_bytes=ALIGN)

        def bank_tile(shape, number):
            return psum.tile(shape, F32, name="bank", tag="bank%d" % number)

        offsets = {
            "head": lists.tile([P, S // LIST_ROWS], U16, name="head_list"),
            "tail": lists.tile([P, S // LIST_ROWS], U16, name="tail_list"),
        }

        wi_scales_raw = held([P, PASSES * H], U8, "wi_scales_raw")
        table_scales = held([P, T], U8, "table_scales")
        for rows, engine in ((slice(0, 16), nc.gpsimd), (slice(32, 48), nc.gpsimd), (slice(64, P), nc.vector)):
            engine.memset(table_scales[rows, :].bitcast(I32), 0)
        nc.gpsimd.memset(wi_scales_raw[:].bitcast(I32), 0)
        wrel_plane = held([P, N], U8, "wrel_plane")
        nc.gpsimd.memset(wrel_plane[:].bitcast(I32), 0)
        gain_cols = held([P, PACK], F32, "gain_cols")
        nc.gpsimd.dma_start(gain_cols[:], gain.rearrange("(p t) -> p t", t=PACK))

        table_words = [held([P, T], U16, "table_words%d" % a) for a in range(PASSES)]
        wi_raw = [held([P, H], I32, "wi_raw%d" % a) for a in range(PASSES)]
        wr_raw = [held([P, PACK, H], F32, "wr_raw%d" % a, at=AT_RAW[a]) for a in range(PASSES)]

        def load_words(a):
            nc.sync.dma_start(table_words[a][:].bitcast(I32), tab_words[a].bitcast(I32))

        def load_wr(a):
            nc.sync.dma_start(wr_raw[a][:], wr[512 * a : 512 * (a + 1), :].rearrange("(p j) c -> p j c", j=PACK))

        def load_wi(a):
            nc.sync.dma_start(wi_raw[a][:], wi_words[a].rearrange("p c i -> p (c i)").bitcast(I32))

        scale_rows = tab_scales.bitcast(I32).rearrange("a (h q r) c -> q (a h) r c", h=2, q=2)
        for q in range(2):
            nc.sync.dma_start(table_scales[32 * q + 16 : 32 * q + 32, :].bitcast(I32), scale_rows[q])
        nc.sync.dma_start(offsets["tail"][:], offs2)
        nc.sync.dma_start(offsets["head"][:], offs)
        load_words(0)
        load_wi(0)
        for q in range(4):
            nc.sync.dma_start(
                wi_scales_raw[32 * q : 32 * q + 4, :].bitcast(I32).rearrange("r (a c) -> r a c", a=PASSES),
                wi_scales[:, 4 * q : 4 * q + 4, :].bitcast(I32).rearrange("a r c -> r a c"),
            )
        load_words(1)
        load_wi(1)

        picked = {}
        planes = {}
        words = {}

        def gather_scales(side, c):
            cols = slice(c * CHUNK // LIST_ROWS, (c + 1) * CHUNK // LIST_ROWS)
            nc.vector.tensor_copy(picked[side, c], table_scales[:].indirect(offsets[side][:, cols]))

        def place_scales(sides, c, a, rows):
            plane = held([P, len(sides), CHUNK], U8, "plane_%s%d_%d" % (sides[0], c, a))
            for h in range(2):
                source = 16 + 8 * a + 4 * h
                nc.sync.dma_start(plane[64 * h : 64 * h + 64].bitcast(I32), rows[source : source + 64].bitcast(I32))
            for i, side in enumerate(sides):
                planes[side, c, a] = plane[:, i, :]

        def later_scales(side, tag):
            rows = held([P, 1, CHUNK], U8, "picked_%s" % side, tag=tag)
            picked[side, 1] = rows[:, 0, :]
            gather_scales(side, 1)
            for a in range(PASSES):
                place_scales([side], 1, a, rows)

        def later_head_scales(half, tag=None, at=None):
            count = CHUNK // 2
            rows = held([P, count], U8, "picked_head%d" % half, tag=tag, at=at)
            first = CHUNK + half * count
            nc.vector.tensor_copy(
                rows[:], table_scales[:].indirect(offsets["head"][:, first // LIST_ROWS : (first + count) // LIST_ROWS])
            )
            for a in range(PASSES):
                if half == 0:
                    planes["head", 1, a] = held([P, CHUNK], U8, "plane_head1_%d" % a)[:]
                for h in range(2):
                    source = 16 + 8 * a + 4 * h
                    nc.sync.dma_start(
                        planes["head", 1, a][64 * h : 64 * h + 64, half * count : (half + 1) * count].bitcast(I32),
                        rows[source : source + 64].bitcast(I32),
                    )

        def gather_words(side, c, a, within=0, count=CHUNK):
            first = c * CHUNK + within
            cols = slice(first // LIST_ROWS, (first + count) // LIST_ROWS)
            nc.vector.tensor_copy(
                words[side, c, a][:, within : within + count], table_words[a][:].indirect(offsets[side][:, cols])
            )

        codes = {"im": held([P, PASSES * H], I32, "wi_codes"), "re": held([P, PASSES * H], I32, "wr_codes")}
        scales = {"im": held([P, PASSES * H], U8, "wi_plane"), "re": held([P, PASSES * H], U8, "wr_plane")}

        def deal_wi(a):
            cols = slice(a * H, (a + 1) * H)
            nc.gpsimd.tensor_copy(
                scales["im"][:, cols].rearrange("p (t g m) -> p g t m", t=PACK, m=16),
                wi_scales_raw[:, cols].rearrange("p (g m t) -> p g t m", t=PACK, m=16),
            )
            nc.scalar.copy(
                codes["im"][:, cols].bitcast(U32).rearrange("p (t g m) -> p g t m", t=PACK, m=4),
                wi_raw[a][:].bitcast(U32).rearrange("p (g m t) -> p g t m", t=PACK, m=4),
            )

        wr_rounded = {}

        def round_wr(a):
            wr_rounded[a] = held([P, PACK * H], BF16, "wr_rounded%d" % a, at=AT_ROUNDED[a])
            rounded = wr_rounded[a][:].rearrange("p (t m j) -> p m t j", t=PACK, j=PACK)
            for first, last, engine in SHARES[a]:
                raw = wr_raw[a][:].rearrange("p j (m t) -> p m t j", t=PACK)[:, first:last]
                share = rounded[:, first:last]
                if engine == "pool":
                    nc.gpsimd.tensor_copy(share, raw)
                else:
                    nc.scalar.copy(share.rearrange("p m t (u v) -> p m u t v", v=2), raw.rearrange("p m t (u v) -> p m u t v", v=2))

        def quantise_wr(a):
            cols = slice(a * H, (a + 1) * H)
            nc.vector.quantize_mx(out=codes["re"][:, cols].bitcast(FP8X4), scales=scales["re"][:, cols], in_=wr_rounded[a][:])

        def weight(part, a, t):
            cols = slice(a * H + t * P, a * H + (t + 1) * P)
            return codes[part][:, cols].bitcast(FP8X4), scales[part][:, cols]

        tail_banks = {}

        def tail_passes(part, c, first_bank, order):
            if (part, c) not in tail_banks:
                tail_banks[part, c] = [bank_tile([P, CHUNK], first_bank + t) for t in range(PACK)]
            for a, t in order:
                w, w_scale = weight(part, a, t)
                nc.tensor.matmul_mx(
                    out=tail_banks[part, c][t][:],
                    lhsT=w,
                    lhsT_scale=w_scale,
                    rhs=words["tail", c, a].bitcast(FP4X4),
                    rhs_scale=planes["tail", c, a],
                    start=(a == 0),
                    stop=(a == PASSES - 1),
                )

        by_pass = [(a, t) for a in range(PASSES) for t in range(PACK)]
        by_slice = [(a, t) for t in range(PACK) for a in range(PASSES)]
        tails = {}

        def tail_copies(part, c, at=None, width=CHUNK):
            tails[part, c] = held([P, PACK, CHUNK], F32, "tail_%s%d" % (part, c), at=at)
            for first in range(0, CHUNK, width):
                cols = slice(first, first + width)
                for t in range(PACK):
                    nc.scalar.activation(
                        tails[part, c][:, t, cols], tail_banks[part, c][t][:, cols], COPY, scale=gain_cols[:, t : t + 1]
                    )

        products = {}
        head_banks = {}

        def head_passes(part, s, number, order=by_slice):
            c, within = divmod(s * STRIP, CHUNK)
            if (part, s) not in head_banks:
                head_banks[part, s] = bank_tile([P, PACK, STRIP], number)
            one_group = len(order) == PACK
            for a, t in order:
                w, w_scale = weight(part, a, t)
                nc.tensor.matmul_mx(
                    out=head_banks[part, s][:, t, :],
                    lhsT=w,
                    lhsT_scale=w_scale,
                    rhs=words["head", c, a][:, within : within + STRIP].bitcast(FP4X4),
                    rhs_scale=planes["head", c, a][:, within : within + STRIP],
                    start=(a == 0 and (t == 0 or not one_group)),
                    stop=(a == PASSES - 1 and (t == PACK - 1 or not one_group)),
                )

        def wide_passes(part, s, u, number, order=None):
            c, within = divmod(s * STRIP, CHUNK)
            if (part, s, u) not in head_banks:
                head_banks[part, s, u] = bank_tile([P, 2, 2 * STRIP], number)
            for a in order or range(PASSES):
                for v in range(2):
                    w, w_scale = weight(part, a, 2 * u + v)
                    nc.tensor.matmul_mx(
                        out=head_banks[part, s, u][:, v, :],
                        lhsT=w,
                        lhsT_scale=w_scale,
                        rhs=words["head", c, a][:, within : within + 2 * STRIP].bitcast(FP4X4),
                        rhs_scale=planes["head", c, a][:, within : within + 2 * STRIP],
                        start=(a == 0 and v == 0),
                        stop=(a == PASSES - 1 and v == 1),
                    )

        def in_pairs(columns, u):
            return columns.rearrange("p (g t i) -> p g t i", i=2, t=PACK)[:, :, 2 * u : 2 * u + 2, :]

        def multiply_wide(part, s, u):
            c, within = divmod(s * STRIP, CHUNK)
            nc.vector.tensor_tensor(
                in_pairs(strips_of(part, s, 2), u),
                head_banks[part, s, u][:].rearrange("p v (g i) -> p g v i", i=2),
                tails[part, c][:, 2 * u : 2 * u + 2, within : within + 2 * STRIP].rearrange("p v (g i) -> p g v i", i=2),
                MULT,
            )

        def product_tile(part, first, count, at=None):
            tile = held([P, PACK * STRIP * count], F32, "products_%s%d" % (part, first), at=at)
            for i in range(count):
                products[part, first + i] = tile[:, PACK * STRIP * i :]

        def strips_of(part, s, count=1):
            return products[part, s][:, : PACK * STRIP * count]

        def multiply(part, s, at=None):
            c, within = divmod(s * STRIP, CHUNK)
            if c:
                product_tile(part, s, 1, at)
            nc.vector.tensor_tensor(
                strips_of(part, s).rearrange("p (g t i) -> p g t i", i=2, t=PACK),
                head_banks[part, s][:].rearrange("p t (g i) -> p g t i", i=2),
                tails[part, c][:, :, within : within + STRIP].rearrange("p t (g i) -> p g t i", i=2),
                MULT,
            )

        def weave_heads(part, s, at):
            woven = held([P, 2 * STRIP * PACK], F32, "heads_%s%d" % (part, s), at=at)
            for u in range(2):
                nc.scalar.copy(in_pairs(woven[:], u), head_banks[part, s, u][:].rearrange("p v (g i) -> p g v i", i=2))
            return woven

        def multiply_on_pool(part, first, count, woven):
            nc.gpsimd.tensor_tensor(
                strips_of(part, first, count).rearrange("p (g t i) -> p g t i", i=2, t=PACK),
                woven[:].rearrange("p (g t i) -> p g t i", i=2, t=PACK),
                tails[part, 0][:, :, STRIP * first : STRIP * (first + count)].rearrange("p t (g i) -> p g t i", i=2),
                MULT,
            )

        def add_on_pool(rounded, s, count):
            nc.gpsimd.tensor_tensor(
                rounded.rearrange("p (g i t) -> p g t i", i=2, t=PACK),
                strips_of("im", s, count).rearrange("p (g t i) -> p g t i", i=2, t=PACK),
                strips_of("re", s, count).rearrange("p (g t i) -> p g t i", i=2, t=PACK),
                ADD,
            )

        def add_products(rounded, s, count, engine):
            engine.tensor_tensor(
                rounded.rearrange("p (g i t) -> p g i t", i=2, t=PACK),
                strips_of("im", s, count).rearrange("p (g t i) -> p g i t", i=2, t=PACK),
                strips_of("re", s, count).rearrange("p (g t i) -> p g i t", i=2, t=PACK),
                ADD,
            )

        quantised = {}

        def quantise_h(first, count, rounded, at=None):
            h_codes = held([P, count], I32, "h_codes%d" % first, at=at)
            h_plane = held([P, count], U8, "h_plane%d" % first)
            nc.vector.quantize_mx(out=h_codes[:].bitcast(FP8X4), scales=h_plane[:], in_=rounded)
            for at in range(0, count, STRIP):
                quantised[first + at] = h_codes[:, at:], h_plane[:, at:]

        def scores(first, count, banks, vector_banks=()):
            h_codes, h_plane = quantised[first]
            tiles = 1 if count == CHUNK else 2
            for n0 in range(0, N // P, tiles):
                bank = bank_tile([P, tiles, count], banks[n0 // tiles])
                for n in range(n0, n0 + tiles):
                    nc.tensor.matmul_mx(
                        out=bank[:, n - n0, :],
                        lhsT=wrel_codes[:, 2 * P * n : 2 * P * (n + 1)].bitcast(FP4X4),
                        lhsT_scale=wrel_plane[:, P * n : P * (n + 1)],
                        rhs=h_codes[:, :count].bitcast(FP8X4),
                        rhs_scale=h_plane[:, :count],
                        start=True,
                        stop=True,
                    )
                result = held([P, tiles, count], F32, "result%d_%d" % (first, n0))
                if n0 // tiles in vector_banks:
                    wide_bias = bias_cols[:, n0 : n0 + tiles].unsqueeze(2).to_broadcast([P, tiles, count])
                    nc.vector.tensor_tensor(result[:], bank[:], wide_bias, ADD)
                else:
                    for n in range(n0, n0 + tiles):
                        nc.scalar.activation(result[:, n - n0, :], bank[:, n - n0, :], IDENTITY, bias=bias_cols[:, n : n + 1])
                step = 1 if count == CHUNK // 2 else tiles
                for n in range(n0, n0 + tiles, step):
                    nc.sync.dma_start(
                        out[n * P : (n + step) * P, first : first + count].rearrange("(n p) j -> p n j", p=P),
                        result[:, n - n0 : n - n0 + step, :],
                    )

        for a in range(PASSES):
            deal_wi(a)
            for side in ("tail", "head"):
                words[side, 0, a] = held([P, CHUNK], U16, "%s_words%d" % (side, a))[:]
        both = held([P, 2, CHUNK], U8, "picked_first")
        for i, side in enumerate(SIDES):
            picked[side, 0] = both[:, i, :]
            gather_scales(side, 0)
        place_scales(["tail"], 0, 0, both[:, :1, :])
        load_wr(0)
        place_scales(SIDES, 0, 1, both)
        place_scales(["head"], 0, 0, both[:, 1:, :])
        load_wr(1)
        for a in range(PASSES):
            gather_words("tail", 0, a)
            gather_words("head", 0, a)
        tail_passes("im", 0, 0, by_pass)
        for s in (0, 2):
            for u in range(2):
                wide_passes("im", s, u, 4 + s + u)
        later_scales("tail", "wi_raw1")
        round_wr(0)
        quantise_wr(0)
        tail_copies("im", 0)
        woven = weave_heads("im", 2, AT_RAW[0] + 1024)
        raw = wr_raw[1][:].rearrange("p j (m t) -> p m t j", t=PACK)
        halves = [held([P, 2, P, PACK], BF16, "wr_rounded1_%d" % u, at=AT_ROUNDED[1] + 1024 + 2048 * u) for u in range(2)]
        nc.gpsimd.tensor_copy(halves[0][:].rearrange("p t m j -> p m t j"), raw[:, :, :2, :])
        nc.scalar.copy(
            halves[1][:].rearrange("p t m (u v) -> p m u t v", v=2), raw[:, :, 2:, :].rearrange("p m t (u v) -> p m u t v", v=2)
        )
        words["tail", 1, 0] = held([P, CHUNK], U16, "tail_words_next0", at=AT_RAW[0])[:]
        gather_words("tail", 1, 0)
        product_tile("im", 0, 2)
        for u in range(2):
            multiply_wide("im", 0, u)
        for u in range(2):
            if u:
                later_head_scales(0, at=AT_ROUNDED[1] + 2048)
            cols = slice(H + u * H // 2, H + (u + 1) * H // 2)
            nc.vector.quantize_mx(
                out=codes["re"][:, cols].bitcast(FP8X4), scales=scales["re"][:, cols], in_=halves[u][:].rearrange("p t m j -> p (t m j)")
            )
        words["tail", 1, 1] = held([P, CHUNK], U16, "tail_words_next1", at=AT_HEAD_PICKED + 1024)[:]
        gather_words("tail", 1, 1)

        wrel_codes = held([P, 2 * N], U8, "wrel_codes")
        nc.sync.dma_start(wrel_codes[:].bitcast(I32), wrel_words[0].bitcast(I32))
        for q in range(4):
            nc.sync.dma_start(
                wrel_plane[32 * q : 32 * q + 4, :].bitcast(I32), wrel_scales[0, 4 * q : 4 * q + 4, :].bitcast(I32)
            )
        bias_cols = held([P, N // P], F32, "bias_cols")
        with nc.allow_non_contiguous_dma(reason="one bias value for each output row"):
            nc.sync.dma_start(bias_cols[:], bias.rearrange("(n p) -> p n", p=P))

        product_tile("im", 2, 2, AT_POOL_PRODUCTS)
        multiply_on_pool("im", 2, 2, woven)
        tail_passes("re", 0, 0, by_pass[:PACK])
        for s, u in ((2, 0), (0, 0), (2, 1), (0, 1)):
            wide_passes("re", s, u, 4 + s + u, [0])
        for u in range(2):
            tail_passes("re", 0, 0, [(1, 2 * u), (1, 2 * u + 1)])
            for s in (0, 2):
                wide_passes("re", s, u, 4 + s + u, [1])
        tail_copies("re", 0, AT_TAIL_RE, CHUNK // 2)
        tail_passes("im", 1, 0, by_slice)
        product_tile("re", 0, 4, AT_PRODUCTS)
        wide = held([P, PACK * CHUNK], BF16, "h_rounded_wide", at=AT_WIDE)
        for s in (0, 2):
            for u in range(2):
                multiply_wide("re", s, u)
            add_on_pool(wide[:, PACK * STRIP * s : PACK * STRIP * (s + 2)], s, 2)
        tail_copies("im", 1)
        tail_passes("re", 1, 4, by_slice)
        tail_copies("re", 1, AT_TAIL_LAST)
        for a in range(PASSES):
            words["head", 1, a] = held([P, CHUNK], U16, "head_words_next%d" % a, at=AT_TAIL_RE + 2 * CHUNK * a)[:]
        for a in range(PASSES):
            gather_words("head", 1, a, 0, CHUNK // 2)
        later_head_scales(1, at=AT_TAIL_RE + 4 * CHUNK)
        for a in range(PASSES):
            gather_words("head", 1, a, CHUNK // 2, CHUNK // 2)
        for s in range(4, 6):
            head_passes("im", s, 2 * (s - 4))
            head_passes("re", s, 2 * (s - 4) + 1)
        for u in range(2):
            wide_passes("im", 6, u, 4 + u)
        for part in ("im", "re"):
            multiply(part, 4)
        quantise_h(0, CHUNK, wide[:])
        middle = held([P, PACK * 256], BF16, "h_rounded_middle", at=AT_WIDE)
        add_on_pool(middle[:, : PACK * STRIP], 4, 1)
        multiply("im", 5, AT_POOL_PRODUCTS + 2048)
        multiply("re", 5, AT_PRODUCTS + 2048)
        for u in range(2):
            wide_passes("re", 6, u, 2 + u)
        add_on_pool(middle[:, PACK * STRIP :], 5, 1)
        product_tile("im", 6, 2, AT_PRODUCTS + 4096)
        for u in range(2):
            multiply_wide("im", 6, u)
        scores(0, CHUNK, (6, 7, 4, 5))
        product_tile("re", 6, 2, AT_TAIL_RE + 4096)
        for u in range(2):
            multiply_wide("re", 6, u)
        quantise_h(512, 256, middle[:], at=AT_TAIL_RE + 2 * CHUNK)
        scores(512, 256, (0, 1))
        last = [held([P, PACK * STRIP], BF16, "h_rounded_last%d" % i, at=AT_TAIL_LAST + 1024 * (i + 1)) for i in range(2)]
        add_products(last[0][:], 6, 1, nc.vector)
        add_products(last[1][:], 7, 1, nc.vector)
        quantise_h(768, 128, last[0][:])
        scores(768, 128, (6, 7), (0,))
        quantise_h(896, 128, last[1][:])
        scores(896, 128, (2, 3), (1,))
